import numpy as np
import ml_dtypes


def mxq(x, axis, fmt="e4m3"):
    dtype, down = {"e4m3": (ml_dtypes.float8_e4m3fn, 7), "e5m2": (ml_dtypes.float8_e5m2, 14)}[fmt]
    v = np.moveaxis(np.asarray(x, np.float32).astype(ml_dtypes.bfloat16).astype(np.float64), axis, -1)
    blocks = v.reshape(v.shape[:-1] + (-1, 32))
    amax = np.abs(blocks).max(-1, keepdims=True)
    byte = np.maximum(np.where(amax > 0, np.frexp(amax)[1] - 1 + 127, 0) - down, 1)
    scale = np.exp2(byte - 127.0)
    codes = (blocks / scale).astype(np.float32).astype(dtype).astype(np.float64)
    return np.moveaxis((codes * scale).reshape(v.shape), -1, axis)


WIDE = False


def mx_kscale(k):
    if not WIDE:
        return np.ones(k)
    levels = np.array([10, -10, 5, -5, 0])
    if k % 512:
        return np.exp2(np.random.permutation(np.resize(levels, k // 32))).repeat(32)
    a = np.empty((k // 512, 16))
    for p in range(k // 512):
        a[p, :8] = np.random.permutation(np.resize(levels, 8))
        for g in range(8):
            far = levels[np.abs(levels - a[p, g]) >= 10]
            a[p, g + 8] = far[np.random.randint(len(far))]
    return np.exp2(a.ravel()).repeat(32)


def f64(x):
    return np.asarray(x).astype(np.float64)


def striped(idx):
    return np.tile(idx.reshape(-1, 16).T, (8, 1)).astype(np.uint16)


def unstriped(offs):
    return offs[:16].T.reshape(-1).astype(np.int64)


def pack_weight(w):
    k, n = w.shape
    w = f64(np.asarray(w, np.float32).astype(ml_dtypes.bfloat16)).reshape(k // 32, 32, n)
    amax = np.abs(w).max(1)
    byte = np.clip(np.where(amax > 0, np.frexp(amax)[1] - 1 + 127 - 7, 1), 1, 254)
    scaled = (w * np.exp2(127.0 - byte)[:, None, :]).reshape(k, n).astype(np.float32)
    words = np.ascontiguousarray(scaled.reshape(k // 512, 128, 4, n).transpose(0, 1, 3, 2)).astype(ml_dtypes.float8_e4m3fn).view(np.uint8)
    return words, np.ascontiguousarray(byte.astype(np.uint8).reshape(k // 512, 16, n))


def unpack_weight(words, scales):
    g, p, n, _ = words.shape
    vals = np.ascontiguousarray(words).view(ml_dtypes.float8_e4m3fn).astype(np.float64) * np.repeat(np.exp2(scales.astype(np.float64) - 127.0), 8, axis=1)[..., None]
    return vals.transpose(0, 1, 3, 2).reshape(g * 512, n)


def planes(y):
    n, m = y.shape
    v = y.astype(np.float32).astype(ml_dtypes.bfloat16).astype(np.float64).reshape(n // 32, 32, m)
    top = np.abs(v).max(1)
    byte = np.clip(np.where(top > 0, np.frexp(top)[1] - 1 + 127 - 7, 1), 1, 254)
    codes = (v * np.exp2(127.0 - byte)[:, None, :]).reshape(n, m).astype(np.float32).astype(ml_dtypes.float8_e4m3fn).view(np.uint8)
    words = codes.reshape(n // 512, 128, 4, m).transpose(0, 1, 3, 2)
    return np.ascontiguousarray(words), np.ascontiguousarray(byte.astype(np.uint8).reshape(n // 512, 16, m))


def relu(v):
    return np.maximum(v, 0.0)


K, T, S, H, N, D = 512, 2048, 1024, 512, 512, 2


def setup_inputs():
    n = np.random.standard_normal
    s = mx_kscale(K)[:, None]
    u = mx_kscale(H)
    packed_xT = pack_weight(n((K, T)) * s)
    return {
        "x_words": packed_xT[0],
        "x_scales": packed_xT[1],
        "w1": (n((K, N)) / np.sqrt(K) / s).astype(np.float32),
        "w2": (n((H, N)) / np.sqrt(H) / u[:, None]).astype(np.float32),
        "gain": (np.random.uniform(0.5, 1.5, (H, 1)) * u[:, None]).astype(np.float32),
        "offs": striped(np.random.permutation(T)[:S]),
    }


def reference(x_words, x_scales, w1, w2, gain, offs):
    xq = unpack_weight(x_words, x_scales)[:, unstriped(offs)]
    y = relu(mxq(f64(w1), 0, "e4m3").T @ xq) + 0.05
    ee = (y * y) * y
    z = f64(gain) * (np.exp((np.log(ee.reshape(len(ee), -1, D).mean(axis=2))) / 3))
    out_0 = mxq(f64(w2), 0, "e4m3").T @ mxq(z, 0, "e4m3")
    return (out_0,) + planes(out_0)

@@ -1,0 +1,210 @@
+from contextlib import ExitStack
+
+import concourse.mybir as mybir
+
+K, T, S, H, N, D = 512, 2048, 1024, 512, 512, 2
+V = S // D
+FLOPS = 2 * K * H * S + 2 * H * N * V
+
+F32 = mybir.dt.float32
+BF16 = mybir.dt.bfloat16
+I32 = mybir.dt.int32
+U32 = mybir.dt.uint32
+U16 = mybir.dt.uint16
+U8 = mybir.dt.uint8
+FP8X4 = mybir.dt.float8_e4m3fn_x4
+ACT = mybir.ActivationFunctionType
+ALU = mybir.AluOpType
+
+P = 128
+PACK = 4
+SHIFT = 0.05
+CHUNKS = 4
+CV = V // CHUNKS
+CJ = CV * D
+BJ = 128
+
+
+def tile_picked_ygem_none_po_kernel(tc, x_words, x_scales, w1, w2, gain, offs, out_0, out_1, out_2):
+    nc = tc.nc
+    with ExitStack() as ctx:
+        keep = ctx.enter_context(tc.tile_pool(name="keep", bufs=1))
+        psum = ctx.enter_context(tc.psum_pool(name="psum", bufs=8))
+
+        offsets = keep.tile([P, S // 16], U16, name="offsets")
+        nc.sync.dma_start(offsets[:], offs)
+
+        scale_table = keep.tile([P, T], U8, name="scale_table", align_bytes=64)
+        nc.vector.memset(scale_table[:].bitcast(I32), 0)
+
+        def load_half(w, name, h):
+            raw = keep.tile([P, PACK, 256], F32, name=f"{name}_raw{h}")
+            nc.sync.dma_start(raw[:], w.rearrange("(p j) c -> p j c", j=PACK)[:, :, 256 * h : 256 * (h + 1)])
+            return raw
+
+        w1_raw = [load_half(w1, "w1", 0)]
+        for q in range(4):
+            nc.sync.dma_start(scale_table[32 * q : 32 * q + 4, :].bitcast(I32), x_scales[0, 4 * q : 4 * q + 4, :].bitcast(I32))
+        w1_raw.append(load_half(w1, "w1", 1))
+        word_table = keep.tile([P, T], U32, name="word_table", align_bytes=64)
+        nc.sync.dma_start(word_table[:].bitcast(I32), x_words[0].rearrange("p n r -> p (n r)").bitcast(I32))
+        w2_raw = [load_half(w2, "w2", h) for h in range(2)]
+        gains = keep.tile([P, PACK], F32, name="gains")
+        nc.sync.dma_start(gains[:], gain.rearrange("(p t) o -> p (t o)", t=PACK))
+
+        ones = keep.tile([P, 1], F32, name="ones")
+        nc.vector.memset(ones[:], 1.0)
+        mean_bias = keep.tile([P, 1], F32, name="mean_bias")
+        nc.scalar.activation(mean_bias[:], ones[:], ACT.Ln, scale=float(D) ** (-1.0 / 3.0))
+
+        def deal(copy, grouped, raw, h, a, b):
+            dst = grouped[:].rearrange("p (t m j) -> p m t j", t=PACK, j=PACK)[:, 64 * h + a : 64 * h + b]
+            src = raw[:].rearrange("p j (m t) -> p m t j", t=PACK)[:, a:b]
+            copy(dst, src)
+
+        x_scale_tiles = []
+        for g in range(2):
+            xs = keep.tile([P, 512], U8, name=f"xs{g}", align_bytes=64)
+            nc.vector.tensor_copy(xs[:], scale_table[:].indirect(offsets[:, 32 * g : 32 * (g + 1)]))
+            x_scale_tiles.append(xs)
+        w1_bf = keep.tile([P, PACK * H], BF16, name="w1_bf", align_bytes=64)
+        deal(nc.scalar.copy, w1_bf, w1_raw[0], 0, 0, 64)
+        deal(nc.scalar.copy, w1_bf, w1_raw[1], 1, 0, 64)
+        w1_codes = keep.tile([P, H], U32, name="w1_codes", align_bytes=64)
+        w1_scales = keep.tile([P, H], U8, name="w1_scales", align_bytes=64)
+        nc.vector.quantize_mx(out=w1_codes[:].bitcast(FP8X4), scales=w1_scales[:], in_=w1_bf[:])
+
+        x_code_tiles = []
+        for c in range(CHUNKS):
+            xc = keep.tile([P, CJ], U32, name=f"xc{c}", align_bytes=64)
+            nc.vector.tensor_copy(xc[:], word_table[:].indirect(offsets[:, 16 * c : 16 * (c + 1)]))
+            x_code_tiles.append(xc)
+
+        sums = keep.tile([P, V * PACK], F32, name="sums", tag="pooled")
+        logs = keep.tile([P, V * PACK], F32, name="logs")
+        pieces = [(0, 2), (2, 4), (4, 6), (6, 7), (7, 8)]
+        piece_of = {b: n for n, (lo, hi) in enumerate(pieces) for b in range(lo, hi)}
+        cubes = [keep.tile([P, (hi - lo) * BJ, PACK], F32, name=f"cubes{lo}") for lo, hi in pieces]
+        odds = [keep.tile([P, (hi - lo) * BJ // D, PACK], F32, name=f"odds{lo}") for lo, hi in pieces]
+
+        def cube(b):
+            c, half = divmod(b, 2)
+            acc = psum.tile([P, PACK, BJ], F32, name="acc")
+            xs = x_scale_tiles[b // 4][:, (b % 4) * BJ : (b % 4 + 1) * BJ]
+            xc = x_code_tiles[c][:, half * BJ : (half + 1) * BJ]
+            for t in range(PACK):
+                nc.tensor.matmul_mx(
+                    out=acc[:, t, :],
+                    lhsT=w1_codes[:, t * P : (t + 1) * P].bitcast(FP8X4),
+                    lhsT_scale=w1_scales[:, t * P : (t + 1) * P],
+                    rhs=xc.bitcast(FP8X4),
+                    rhs_scale=xs,
+                    start=True,
+                    stop=True,
+                )
+            woven = acc[:].rearrange("p t j -> p j t")
+            sq = keep.tile([P, BJ, PACK], F32, name=f"sq{b}")
+            nc.scalar.activation(sq[:], woven, ACT.Square, bias=SHIFT)
+            n = piece_of[b]
+            at = (b - pieces[n][0]) * BJ
+            nc.vector.scalar_tensor_tensor(cubes[n][:, at : at + BJ, :], woven, SHIFT, sq[:], ALU.add, ALU.mult)
+
+        def floor_odd(n):
+            pairs = cubes[n][:].rearrange("p (v e) t -> p v e t", e=D)
+            if n < 3:
+                nc.scalar.activation(odds[n][:], pairs[:, :, 1, :], ACT.Relu, bias=-(SHIFT**3))
+            else:
+                nc.vector.tensor_scalar(odds[n][:], pairs[:, :, 1, :], -(SHIFT**3), 0.0, ALU.add, ALU.max)
+
+        def pool_pairs(n):
+            pairs = cubes[n][:].rearrange("p (v e) t -> p v e t", e=D)
+            lo, hi = pieces[n]
+            cols = slice(lo * BJ // D * PACK, hi * BJ // D * PACK)
+            nc.vector.scalar_tensor_tensor(
+                sums[:, cols].rearrange("p (v t) -> p v t", t=PACK), pairs[:, :, 0, :], SHIFT**3, odds[n][:], ALU.max, ALU.add
+            )
+            nc.scalar.activation(logs[:, cols], sums[:, cols], ACT.Ln, bias=SHIFT**3)
+
+        for b in range(3):
+            cube(b)
+        floor_odd(0)
+        cube(3)
+        cube(4)
+        floor_odd(1)
+        pool_pairs(0)
+        cube(5)
+        cube(6)
+        floor_odd(2)
+        pool_pairs(1)
+        cube(7)
+        floor_odd(3)
+        pool_pairs(2)
+        floor_odd(4)
+        pool_pairs(3)
+        pool_pairs(4)
+
+        w2_bf = keep.tile([P, PACK * N], BF16, name="w2_bf", align_bytes=64)
+        for h in range(2):
+            deal(nc.vector.tensor_copy, w2_bf, w2_raw[h], h, 0, 64)
+        w2_codes = keep.tile([P, N], U32, name="w2_codes", align_bytes=64)
+        w2_scales = keep.tile([P, N], U8, name="w2_scales", align_bytes=64)
+        nc.vector.quantize_mx(out=w2_codes[:].bitcast(FP8X4), scales=w2_scales[:], in_=w2_bf[:])
+
+        roots = keep.tile([P, V * PACK], F32, name="roots", tag="pooled")
+        out_scales = keep.tile([P, V], U8, name="out_scales", align_bytes=64)
+        out_rows = out_0.rearrange("(p t) v -> p t v", t=PACK)
+        out_words = out_1[0].rearrange("p c r -> p (c r)")
+        edges = [0, 64, 192, 320, 448, 512]
+        spans = list(zip(edges[:-1], edges[1:]))
+        z_bf = [keep.tile([P, (hi - lo) * PACK], BF16, name=f"z_bf{lo}", align_bytes=64) for lo, hi in spans]
+        res = [keep.tile([P, PACK, hi - lo], F32, name=f"res{lo}") for lo, hi in spans]
+        res_bf = [keep.tile([P, (hi - lo) * PACK], BF16, name=f"res_bf{lo}", align_bytes=64) for lo, hi in spans]
+
+        def root(c):
+            lo, hi = spans[c]
+            cols = slice(lo * PACK, hi * PACK)
+            nc.scalar.activation(roots[:, cols], logs[:, cols], ACT.Exp, bias=mean_bias[:], scale=1.0 / 3.0)
+            nc.vector.tensor_tensor(
+                z_bf[c][:].rearrange("p (v t) -> p v t", t=PACK),
+                roots[:, cols].rearrange("p (v t) -> p v t", t=PACK),
+                gains[:].unsqueeze(1).to_broadcast([P, hi - lo, PACK]),
+                ALU.mult,
+            )
+
+        def whiten(c):
+            lo, hi = spans[c]
+            zc = keep.tile([P, hi - lo], U32, name=f"zc{c}", align_bytes=64)
+            zs = keep.tile([P, hi - lo], U8, name=f"zs{c}", align_bytes=64)
+            nc.vector.quantize_mx(out=zc[:].bitcast(FP8X4), scales=zs[:], in_=z_bf[c][:])
+            acc = psum.tile([P, PACK, hi - lo], F32, name="acc")
+            for t in range(PACK):
+                nc.tensor.matmul_mx(
+                    out=acc[:, t, :],
+                    lhsT=w2_codes[:, t * P : (t + 1) * P].bitcast(FP8X4),
+                    lhsT_scale=w2_scales[:, t * P : (t + 1) * P],
+                    rhs=zc[:].bitcast(FP8X4),
+                    rhs_scale=zs[:],
+                    start=True,
+                    stop=True,
+                )
+            nc.scalar.copy(res[c][:], acc[:])
+            nc.sync.dma_start(out_rows[:, :, lo:hi], res[c][:])
+
+        def weave(c):
+            nc.vector.tensor_copy(res_bf[c][:].rearrange("p (v t) -> p v t", t=PACK), res[c][:].rearrange("p t v -> p v t"))
+
+        def hand_on(c):
+            lo, hi = spans[c]
+            oc = keep.tile([P, hi - lo], U32, name=f"oc{c}", align_bytes=64)
+            nc.vector.quantize_mx(out=oc[:].bitcast(FP8X4), scales=out_scales[:, lo:hi], in_=res_bf[c][:])
+            nc.sync.dma_start(out_words[:, lo * PACK : hi * PACK].bitcast(I32), oc[:].bitcast(I32))
+
+        stages = [root, whiten, weave, hand_on]
+        for step in range(len(spans) + len(stages) - 1):
+            for s, stage in enumerate(stages):
+                if 0 <= step - s < len(spans):
+                    stage(step - s)
+
+        for q in range(4):
+            queue = nc.scalar if q % 2 else nc.sync
+            queue.dma_start(out_2[0, 4 * q : 4 * q + 4, :].bitcast(I32), out_scales[32 * q : 32 * q + 4, :].bitcast(I32))

@@ -19,6 +19,7 @@ ALU = mybir.AluOpType
 P = 128
 PACK = 4
 SHIFT = 0.05
+F32_MAX = 3.4028234663852886e38
 CHUNKS = 4
 CV = V // CHUNKS
 CJ = CV * D
@@ -84,7 +85,7 @@ def tile_picked_ygem_none_po_kernel(tc, x_words, x_scales, w1, w2, gain, offs, o
         logs = keep.tile([P, V * PACK], F32, name="logs")
         pieces = [(0, 2), (2, 4), (4, 6), (6, 7), (7, 8)]
         piece_of = {b: n for n, (lo, hi) in enumerate(pieces) for b in range(lo, hi)}
-        cubes = [keep.tile([P, (hi - lo) * BJ, PACK], F32, name=f"cubes{lo}") for lo, hi in pieces]
+        cubes = [keep.tile([P, (hi - lo) * BJ, PACK], F32, name=f"cubes{lo}", tag=f"cubes{lo}", align_bytes=64) for lo, hi in pieces]
         odds = [keep.tile([P, (hi - lo) * BJ // D, PACK], F32, name=f"odds{lo}") for lo, hi in pieces]
 
         def cube(b):
@@ -111,10 +112,10 @@ def tile_picked_ygem_none_po_kernel(tc, x_words, x_scales, w1, w2, gain, offs, o
 
         def floor_odd(n):
             pairs = cubes[n][:].rearrange("p (v e) t -> p v e t", e=D)
-            if n < 3:
-                nc.scalar.activation(odds[n][:], pairs[:, :, 1, :], ACT.Relu, bias=-(SHIFT**3))
+            if n < 4:
+                nc.gpsimd.tensor_scalar(odds[n][:], pairs[:, :, 1, :], F32_MAX, SHIFT**3, ALU.min, ALU.max)
             else:
-                nc.vector.tensor_scalar(odds[n][:], pairs[:, :, 1, :], -(SHIFT**3), 0.0, ALU.add, ALU.max)
+                nc.vector.tensor_scalar(odds[n][:], pairs[:, :, 1, :], SHIFT**3, None, ALU.max)
 
         def pool_pairs(n):
             pairs = cubes[n][:].rearrange("p (v e) t -> p v e t", e=D)
@@ -123,27 +124,22 @@ def tile_picked_ygem_none_po_kernel(tc, x_words, x_scales, w1, w2, gain, offs, o
             nc.vector.scalar_tensor_tensor(
                 sums[:, cols].rearrange("p (v t) -> p v t", t=PACK), pairs[:, :, 0, :], SHIFT**3, odds[n][:], ALU.max, ALU.add
             )
-            nc.scalar.activation(logs[:, cols], sums[:, cols], ACT.Ln, bias=SHIFT**3)
+            nc.scalar.activation(logs[:, cols], sums[:, cols], ACT.Ln)
 
-        for b in range(3):
-            cube(b)
-        floor_odd(0)
-        cube(3)
-        cube(4)
-        floor_odd(1)
-        pool_pairs(0)
-        cube(5)
-        cube(6)
-        floor_odd(2)
-        pool_pairs(1)
-        cube(7)
-        floor_odd(3)
-        pool_pairs(2)
+        cube(0)
+        cube(1)
+        for n in range(3):
+            floor_odd(n)
+            cube(2 * n + 2)
+            if n == 2:
+                floor_odd(3)
+            cube(2 * n + 3)
+            pool_pairs(n)
         floor_odd(4)
         pool_pairs(3)
         pool_pairs(4)
 
-        w2_bf = keep.tile([P, PACK * N], BF16, name="w2_bf", align_bytes=64)
+        w2_bf = keep.tile([P, PACK * N], BF16, name="w2_bf", tag="cubes7", align_bytes=64)
         for h in range(2):
             deal(nc.vector.tensor_copy, w2_bf, w2_raw[h], h, 0, 64)
         w2_codes = keep.tile([P, N], U32, name="w2_codes", align_bytes=64)
@@ -156,7 +152,9 @@ def tile_picked_ygem_none_po_kernel(tc, x_words, x_scales, w1, w2, gain, offs, o
         out_words = out_1[0].rearrange("p c r -> p (c r)")
         edges = [0, 64, 192, 320, 448, 512]
         spans = list(zip(edges[:-1], edges[1:]))
-        z_bf = [keep.tile([P, (hi - lo) * PACK], BF16, name=f"z_bf{lo}", align_bytes=64) for lo, hi in spans]
+        z_all = keep.tile([P, V * PACK], BF16, name="z_all", tag="cubes7", align_bytes=64)
+        z_bf = [z_all[:, lo * PACK : hi * PACK] for lo, hi in spans]
+        out_codes = keep.tile([P, V], U32, name="out_codes", align_bytes=64)
         res = [keep.tile([P, PACK, hi - lo], F32, name=f"res{lo}") for lo, hi in spans]
         res_bf = [keep.tile([P, (hi - lo) * PACK], BF16, name=f"res_bf{lo}", align_bytes=64) for lo, hi in spans]
 
@@ -165,7 +163,7 @@ def tile_picked_ygem_none_po_kernel(tc, x_words, x_scales, w1, w2, gain, offs, o
             cols = slice(lo * PACK, hi * PACK)
             nc.scalar.activation(roots[:, cols], logs[:, cols], ACT.Exp, bias=mean_bias[:], scale=1.0 / 3.0)
             nc.vector.tensor_tensor(
-                z_bf[c][:].rearrange("p (v t) -> p v t", t=PACK),
+                z_bf[c].rearrange("p (v t) -> p v t", t=PACK),
                 roots[:, cols].rearrange("p (v t) -> p v t", t=PACK),
                 gains[:].unsqueeze(1).to_broadcast([P, hi - lo, PACK]),
                 ALU.mult,
@@ -175,7 +173,7 @@ def tile_picked_ygem_none_po_kernel(tc, x_words, x_scales, w1, w2, gain, offs, o
             lo, hi = spans[c]
             zc = keep.tile([P, hi - lo], U32, name=f"zc{c}", align_bytes=64)
             zs = keep.tile([P, hi - lo], U8, name=f"zs{c}", align_bytes=64)
-            nc.vector.quantize_mx(out=zc[:].bitcast(FP8X4), scales=zs[:], in_=z_bf[c][:])
+            nc.vector.quantize_mx(out=zc[:].bitcast(FP8X4), scales=zs[:], in_=z_bf[c])
             acc = psum.tile([P, PACK, hi - lo], F32, name="acc")
             for t in range(PACK):
                 nc.tensor.matmul_mx(
@@ -195,9 +193,10 @@ def tile_picked_ygem_none_po_kernel(tc, x_words, x_scales, w1, w2, gain, offs, o
 
         def hand_on(c):
             lo, hi = spans[c]
-            oc = keep.tile([P, hi - lo], U32, name=f"oc{c}", align_bytes=64)
-            nc.vector.quantize_mx(out=oc[:].bitcast(FP8X4), scales=out_scales[:, lo:hi], in_=res_bf[c][:])
-            nc.sync.dma_start(out_words[:, lo * PACK : hi * PACK].bitcast(I32), oc[:].bitcast(I32))
+            nc.vector.quantize_mx(out=out_codes[:, lo:hi].bitcast(FP8X4), scales=out_scales[:, lo:hi], in_=res_bf[c][:])
+            if c in (2, 4):
+                first = 0 if c == 2 else spans[3][0]
+                nc.sync.dma_start(out_words[:, first * PACK : hi * PACK].bitcast(I32), out_codes[:, first:hi].bitcast(I32))
 
         stages = [root, whiten, weave, hand_on]
         for step in range(len(spans) + len(stages) - 1):

@@ -76,10 +76,10 @@ def tile_picked_ygem_none_po_kernel(tc, x_words, x_scales, w1, w2, gain, offs, o
         nc.vector.quantize_mx(out=w1_codes[:].bitcast(FP8X4), scales=w1_scales[:], in_=w1_bf[:])
 
         x_code_tiles = []
-        for c in range(CHUNKS):
-            xc = keep.tile([P, CJ], U32, name=f"xc{c}", align_bytes=64)
-            nc.vector.tensor_copy(xc[:], word_table[:].indirect(offsets[:, 16 * c : 16 * (c + 1)]))
-            x_code_tiles.append(xc)
+        for lo, hi in [(0, 256), (256, 512), (512, 1024)]:
+            xc = keep.tile([P, hi - lo], U32, name=f"xc{lo}", align_bytes=64)
+            nc.vector.tensor_copy(xc[:], word_table[:].indirect(offsets[:, lo // 16 : hi // 16]))
+            x_code_tiles.extend(xc[:, at : at + BJ] for at in range(0, hi - lo, BJ))
 
         sums = keep.tile([P, V * PACK], F32, name="sums", tag="pooled")
         logs = keep.tile([P, V * PACK], F32, name="logs")
@@ -89,10 +89,9 @@ def tile_picked_ygem_none_po_kernel(tc, x_words, x_scales, w1, w2, gain, offs, o
         odds = [keep.tile([P, (hi - lo) * BJ // D, PACK], F32, name=f"odds{lo}") for lo, hi in pieces]
 
         def cube(b):
-            c, half = divmod(b, 2)
             acc = psum.tile([P, PACK, BJ], F32, name="acc")
             xs = x_scale_tiles[b // 4][:, (b % 4) * BJ : (b % 4 + 1) * BJ]
-            xc = x_code_tiles[c][:, half * BJ : (half + 1) * BJ]
+            xc = x_code_tiles[b]
             for t in range(PACK):
                 nc.tensor.matmul_mx(
                     out=acc[:, t, :],
@@ -121,10 +120,8 @@ def tile_picked_ygem_none_po_kernel(tc, x_words, x_scales, w1, w2, gain, offs, o
             pairs = cubes[n][:].rearrange("p (v e) t -> p v e t", e=D)
             lo, hi = pieces[n]
             cols = slice(lo * BJ // D * PACK, hi * BJ // D * PACK)
-            nc.vector.scalar_tensor_tensor(
-                sums[:, cols].rearrange("p (v t) -> p v t", t=PACK), pairs[:, :, 0, :], SHIFT**3, odds[n][:], ALU.max, ALU.add
-            )
-            nc.scalar.activation(logs[:, cols], sums[:, cols], ACT.Ln)
+            total = sums[:, cols].rearrange("p (v t) -> p v t", t=PACK)
+            nc.vector.scalar_tensor_tensor(total, pairs[:, :, 0, :], SHIFT**3, odds[n][:], ALU.max, ALU.add)
 
         cube(0)
         cube(1)
@@ -138,6 +135,9 @@ def tile_picked_ygem_none_po_kernel(tc, x_words, x_scales, w1, w2, gain, offs, o
         floor_odd(4)
         pool_pairs(3)
         pool_pairs(4)
+        for lo, hi in pieces:
+            cols = slice(lo * BJ // D * PACK, hi * BJ // D * PACK)
+            nc.scalar.activation(logs[:, cols], sums[:, cols], ACT.Ln)
 
         w2_bf = keep.tile([P, PACK * N], BF16, name="w2_bf", tag="cubes7", align_bytes=64)
         for h in range(2):
@@ -154,14 +154,22 @@ def tile_picked_ygem_none_po_kernel(tc, x_words, x_scales, w1, w2, gain, offs, o
         spans = list(zip(edges[:-1], edges[1:]))
         z_all = keep.tile([P, V * PACK], BF16, name="z_all", tag="cubes7", align_bytes=64)
         z_bf = [z_all[:, lo * PACK : hi * PACK] for lo, hi in spans]
-        out_codes = keep.tile([P, V], U32, name="out_codes", align_bytes=64)
-        res = [keep.tile([P, PACK, hi - lo], F32, name=f"res{lo}") for lo, hi in spans]
-        res_bf = [keep.tile([P, (hi - lo) * PACK], BF16, name=f"res_bf{lo}", align_bytes=64) for lo, hi in spans]
+        tail_lo = spans[3][0]
+        res_tail = keep.tile([P, PACK, V - tail_lo], F32, name="res_tail")
+        res = [keep.tile([P, PACK, hi - lo], F32, name=f"res{lo}")[:] for lo, hi in spans[:3]]
+        res.extend(res_tail[:, :, lo - tail_lo : hi - tail_lo] for lo, hi in spans[3:])
+        res_bf = keep.tile([P, V * PACK], BF16, name="res_bf", align_bytes=64)
+
+        last = len(spans) - 1
 
         def root(c):
             lo, hi = spans[c]
             cols = slice(lo * PACK, hi * PACK)
             nc.scalar.activation(roots[:, cols], logs[:, cols], ACT.Exp, bias=mean_bias[:], scale=1.0 / 3.0)
+
+        def apply_gain(c):
+            lo, hi = spans[c]
+            cols = slice(lo * PACK, hi * PACK)
             nc.vector.tensor_tensor(
                 z_bf[c].rearrange("p (v t) -> p v t", t=PACK),
                 roots[:, cols].rearrange("p (v t) -> p v t", t=PACK),
@@ -185,24 +193,43 @@ def tile_picked_ygem_none_po_kernel(tc, x_words, x_scales, w1, w2, gain, offs, o
                     start=True,
                     stop=True,
                 )
-            nc.scalar.copy(res[c][:], acc[:])
-            nc.sync.dma_start(out_rows[:, :, lo:hi], res[c][:])
+            nc.scalar.copy(res[c], acc[:])
+            if c < 3:
+                nc.sync.dma_start(out_rows[:, :, lo:hi], res[c])
+            if c == last:
+                nc.sync.dma_start(out_rows[:, :, tail_lo:V], res_tail[:])
+                weave(nc.scalar.copy, c, acc[:])
 
-        def weave(c):
-            nc.vector.tensor_copy(res_bf[c][:].rearrange("p (v t) -> p v t", t=PACK), res[c][:].rearrange("p t v -> p v t"))
+        def weave(copy, c, source):
+            lo, hi = spans[c]
+            copy(res_bf[:, lo * PACK : hi * PACK].rearrange("p (v t) -> p v t", t=PACK), source.rearrange("p t v -> p v t"))
+
+        split = spans[3][0]
+        early_codes = keep.tile([P, split], U32, name="early_codes", align_bytes=64)
+        late_codes = keep.tile([P, V - split], U32, name="late_codes", align_bytes=64)
 
         def hand_on(c):
             lo, hi = spans[c]
-            nc.vector.quantize_mx(out=out_codes[:, lo:hi].bitcast(FP8X4), scales=out_scales[:, lo:hi], in_=res_bf[c][:])
-            if c in (2, 4):
-                first = 0 if c == 2 else spans[3][0]
-                nc.sync.dma_start(out_words[:, first * PACK : hi * PACK].bitcast(I32), out_codes[:, first:hi].bitcast(I32))
+            codes, first = (early_codes, 0) if hi <= split else (late_codes, split)
+            nc.vector.quantize_mx(
+                out=codes[:, lo - first : hi - first].bitcast(FP8X4), scales=out_scales[:, lo:hi], in_=res_bf[:, lo * PACK : hi * PACK]
+            )
+            if c in (2, 3):
+                nc.sync.dma_start(out_words[:, first * PACK : (first + codes.shape[1]) * PACK].bitcast(I32), codes[:].bitcast(I32))
 
-        stages = [root, whiten, weave, hand_on]
-        for step in range(len(spans) + len(stages) - 1):
-            for s, stage in enumerate(stages):
-                if 0 <= step - s < len(spans):
-                    stage(step - s)
+        for c in range(len(spans)):
+            root(c)
+        for c in range(len(spans)):
+            apply_gain(c)
+            if c > 0:
+                whiten(c - 1)
+        whiten(last)
+        for c in range(last):
+            weave(nc.vector.tensor_copy, c, res[c])
+            if c > 0:
+                hand_on(c - 1)
+        hand_on(last)
+        hand_on(last - 1)
 
         for q in range(4):
             queue = nc.scalar if q % 2 else nc.sync

@@ -24,6 +24,7 @@ CHUNKS = 4
 CV = V // CHUNKS
 CJ = CV * D
 BJ = 128
+WARM_UPS = 3
 
 
 def tile_picked_ygem_none_po_kernel(tc, x_words, x_scales, w1, w2, gain, offs, out_0, out_1, out_2):
@@ -49,7 +50,8 @@ def tile_picked_ygem_none_po_kernel(tc, x_words, x_scales, w1, w2, gain, offs, o
         w1_raw.append(load_half(w1, "w1", 1))
         word_table = keep.tile([P, T], U32, name="word_table", align_bytes=64)
         nc.sync.dma_start(word_table[:].bitcast(I32), x_words[0].rearrange("p n r -> p (n r)").bitcast(I32))
-        w2_raw = [load_half(w2, "w2", h) for h in range(2)]
+        w2_raw = keep.tile([P, PACK, N], F32, name="w2_raw")
+        nc.sync.dma_start(w2_raw[:], w2.rearrange("(p j) c -> p j c", j=PACK))
         gains = keep.tile([P, PACK], F32, name="gains")
         nc.sync.dma_start(gains[:], gain.rearrange("(p t) o -> p (t o)", t=PACK))
 
@@ -140,11 +142,27 @@ def tile_picked_ygem_none_po_kernel(tc, x_words, x_scales, w1, w2, gain, offs, o
             nc.scalar.activation(logs[:, cols], sums[:, cols], ACT.Ln)
 
         w2_bf = keep.tile([P, PACK * N], BF16, name="w2_bf", tag="cubes7", align_bytes=64)
-        for h in range(2):
-            deal(nc.vector.tensor_copy, w2_bf, w2_raw[h], h, 0, 64)
         w2_codes = keep.tile([P, N], U32, name="w2_codes", align_bytes=64)
         w2_scales = keep.tile([P, N], U8, name="w2_scales", align_bytes=64)
-        nc.vector.quantize_mx(out=w2_codes[:].bitcast(FP8X4), scales=w2_scales[:], in_=w2_bf[:])
+        w2_dst = w2_bf[:].rearrange("p (t m j) -> p m t j", t=PACK, j=PACK)
+        w2_src = w2_raw[:].rearrange("p j (m t) -> p m t j", t=PACK)
+        for u in range(2):
+            nc.vector.tensor_copy(w2_dst[:, :, 2 * u : 2 * u + 2], w2_src[:, :, 2 * u : 2 * u + 2])
+        for u in range(2):
+            cols = slice(256 * u, 256 * (u + 1))
+            nc.vector.quantize_mx(out=w2_codes[:, cols].bitcast(FP8X4), scales=w2_scales[:, cols], in_=w2_bf[:, 1024 * u : 1024 * (u + 1)])
+
+        idle = psum.tile([P, 512], F32, name="acc")
+        for n in range(WARM_UPS):
+            nc.tensor.matmul_mx(
+                out=idle[:],
+                lhsT=w2_codes[:, 0:P].bitcast(FP8X4),
+                lhsT_scale=w2_scales[:, 0:P],
+                rhs=w1_codes[:].bitcast(FP8X4),
+                rhs_scale=w1_scales[:],
+                start=True,
+                stop=True,
+            )
 
         roots = keep.tile([P, V * PACK], F32, name="roots", tag="pooled")
         out_scales = keep.tile([P, V], U8, name="out_scales", align_bytes=64)

@@ -1,6 +1,7 @@
 from contextlib import ExitStack
 
 import concourse.mybir as mybir
+from concourse.masks import make_identity
 
 K, T, S, H, N, D = 512, 2048, 1024, 512, 512, 2
 V = S // D
@@ -86,9 +87,15 @@ def tile_picked_ygem_none_po_kernel(tc, x_words, x_scales, w1, w2, gain, offs, o
         sums = keep.tile([P, V * PACK], F32, name="sums", tag="pooled")
         logs = keep.tile([P, V * PACK], F32, name="logs")
         pieces = [(0, 2), (2, 4), (4, 6), (6, 7), (7, 8)]
+        sum_ranges = [(0, 2), (2, 4), (4, 5), (5, 6), (6, 7), (7, 8)]
         piece_of = {b: n for n, (lo, hi) in enumerate(pieces) for b in range(lo, hi)}
-        cubes = [keep.tile([P, (hi - lo) * BJ, PACK], F32, name=f"cubes{lo}", tag=f"cubes{lo}", align_bytes=64) for lo, hi in pieces]
-        odds = [keep.tile([P, (hi - lo) * BJ // D, PACK], F32, name=f"odds{lo}") for lo, hi in pieces]
+        cubes = {n: keep.tile([P, (hi - lo) * BJ, PACK], F32, name=f"cubes{lo}", tag=f"cubes{lo}", align_bytes=64) for n, (lo, hi) in enumerate(pieces) if n > 0}
+        odds = {n: keep.tile([P, (hi - lo) * BJ // D, PACK], F32, name=f"odds{lo}") for n, (lo, hi) in enumerate(pieces) if n > 0}
+
+        parted_cubes = keep.tile([P, D, PACK, P], F32, name="parted_cubes")
+        floored = keep.tile([P, D, PACK, P], F32, name="floored")
+        identity = keep.tile([P, P], F32, name="identity")
+        make_identity(nc, identity[:])
 
         def cube(b):
             acc = psum.tile([P, PACK, BJ], F32, name="acc")
@@ -104,6 +111,14 @@ def tile_picked_ygem_none_po_kernel(tc, x_words, x_scales, w1, w2, gain, offs, o
                     start=True,
                     stop=True,
                 )
+            if b < 2:
+                parted = acc[:].rearrange("p t (v e) -> p e t v", e=D)
+                sq = keep.tile([P, D, PACK, BJ // D], F32, name=f"sq{b}")
+                nc.scalar.activation(sq[:], parted, ACT.Square, bias=SHIFT)
+                images = slice(b * BJ // D, (b + 1) * BJ // D)
+                nc.vector.scalar_tensor_tensor(parted_cubes[:, :, :, images], parted, SHIFT, sq[:], ALU.add, ALU.mult)
+                nc.gpsimd.tensor_scalar(floored[:, :, :, images], parted_cubes[:, :, :, images], F32_MAX, SHIFT**3, ALU.min, ALU.max)
+                return
             woven = acc[:].rearrange("p t j -> p j t")
             sq = keep.tile([P, BJ, PACK], F32, name=f"sq{b}")
             nc.scalar.activation(sq[:], woven, ACT.Square, bias=SHIFT)
@@ -113,33 +128,51 @@ def tile_picked_ygem_none_po_kernel(tc, x_words, x_scales, w1, w2, gain, offs, o
 
         def floor_odd(n):
             pairs = cubes[n][:].rearrange("p (v e) t -> p v e t", e=D)
-            if n < 4:
+            if n == 3:
+                nc.scalar.activation(odds[n][:], pairs[:, :, 1, :], ACT.Relu, bias=-(SHIFT**3))
+            elif n < 3:
                 nc.gpsimd.tensor_scalar(odds[n][:], pairs[:, :, 1, :], F32_MAX, SHIFT**3, ALU.min, ALU.max)
             else:
                 nc.vector.tensor_scalar(odds[n][:], pairs[:, :, 1, :], SHIFT**3, None, ALU.max)
 
-        def pool_pairs(n):
+        def pool_pairs(lo, hi):
+            n = piece_of[lo]
+            first = pieces[n][0]
+            images = slice((lo - first) * BJ // D, (hi - first) * BJ // D)
             pairs = cubes[n][:].rearrange("p (v e) t -> p v e t", e=D)
-            lo, hi = pieces[n]
             cols = slice(lo * BJ // D * PACK, hi * BJ // D * PACK)
             total = sums[:, cols].rearrange("p (v t) -> p v t", t=PACK)
-            nc.vector.scalar_tensor_tensor(total, pairs[:, :, 0, :], SHIFT**3, odds[n][:], ALU.max, ALU.add)
+            nc.vector.scalar_tensor_tensor(total, pairs[:, images, 0, :], SHIFT**3, odds[n][:, images, :], ALU.max, ALU.add)
 
         cube(0)
         cube(1)
-        for n in range(3):
-            floor_odd(n)
-            cube(2 * n + 2)
-            if n == 2:
-                floor_odd(3)
-            cube(2 * n + 3)
-            pool_pairs(n)
+        cube(2)
+        cube(3)
+        floor_odd(1)
+        cube(4)
+        cube(5)
+        pool_pairs(2, 4)
+        floor_odd(2)
+        cube(6)
+        floor_odd(3)
+        cube(7)
+        pool_pairs(4, 5)
+        pool_pairs(5, 6)
         floor_odd(4)
-        pool_pairs(3)
-        pool_pairs(4)
-        for lo, hi in pieces:
+        pool_pairs(6, 7)
+        pool_pairs(7, 8)
+        turned_sums = psum.tile([P, PACK, P], F32, name="acc")
+        for t in range(PACK):
+            for e in range(D):
+                nc.tensor.matmul(turned_sums[:, t, :], floored[:, e, t, :], identity[:], start=e == 0, stop=e == D - 1, is_transpose=True)
+        turned_logs = keep.tile([P, PACK, P], F32, name="turned_logs")
+        nc.scalar.activation(turned_logs[:], turned_sums[:], ACT.Ln)
+        first_logs = psum.tile([P, PACK, P], F32, name="acc")
+        for t in range(PACK):
+            nc.tensor.transpose(first_logs[:, t, :], turned_logs[:, t, :], identity[:])
+        for lo, hi in sum_ranges[1:]:
             cols = slice(lo * BJ // D * PACK, hi * BJ // D * PACK)
-            nc.scalar.activation(logs[:, cols], sums[:, cols], ACT.Ln)
+            nc.scalar.activation(logs[:, cols], sums[:, cols], ACT.Ln, bias=SHIFT**3 if lo == 6 else 0.0)
 
         w2_bf = keep.tile([P, PACK * N], BF16, name="w2_bf", tag="cubes7", align_bytes=64)
         w2_codes = keep.tile([P, N], U32, name="w2_codes", align_bytes=64)
@@ -182,14 +215,19 @@ def tile_picked_ygem_none_po_kernel(tc, x_words, x_scales, w1, w2, gain, offs, o
 
         def root(c):
             lo, hi = spans[c]
-            cols = slice(lo * PACK, hi * PACK)
-            nc.scalar.activation(roots[:, cols], logs[:, cols], ACT.Exp, bias=mean_bias[:], scale=1.0 / 3.0)
+            if lo < P:
+                top = min(hi, P)
+                woven = first_logs[:].rearrange("p t v -> p v t")[:, lo:top]
+                nc.scalar.activation(roots[:, lo * PACK : top * PACK].rearrange("p (v t) -> p v t", t=PACK), woven, ACT.Exp, bias=mean_bias[:], scale=1.0 / 3.0)
+                lo = top
+            if lo < hi:
+                cols = slice(lo * PACK, hi * PACK)
+                nc.scalar.activation(roots[:, cols], logs[:, cols], ACT.Exp, bias=mean_bias[:], scale=1.0 / 3.0)
 
-        def apply_gain(c):
-            lo, hi = spans[c]
+        def apply_gain(lo, hi):
             cols = slice(lo * PACK, hi * PACK)
             nc.vector.tensor_tensor(
-                z_bf[c].rearrange("p (v t) -> p v t", t=PACK),
+                z_all[:, cols].rearrange("p (v t) -> p v t", t=PACK),
                 roots[:, cols].rearrange("p (v t) -> p v t", t=PACK),
                 gains[:].unsqueeze(1).to_broadcast([P, hi - lo, PACK]),
                 ALU.mult,
@@ -237,10 +275,15 @@ def tile_picked_ygem_none_po_kernel(tc, x_words, x_scales, w1, w2, gain, offs, o
 
         for c in range(len(spans)):
             root(c)
-        for c in range(len(spans)):
-            apply_gain(c)
-            if c > 0:
-                whiten(c - 1)
+        apply_gain(0, 64)
+        whiten(0)
+        apply_gain(64, 192)
+        for c in range(1, last):
+            hi = spans[c][1]
+            if c > 1:
+                apply_gain(hi - 64, hi)
+            apply_gain(hi, hi + 64)
+            whiten(c)
         whiten(last)
         for c in range(last):
             weave(nc.vector.tensor_copy, c, res[c])

@@ -26,6 +26,7 @@ CV = V // CHUNKS
 CJ = CV * D
 BJ = 128
 WARM_UPS = 3
+LINE = 4
 
 
 def tile_picked_ygem_none_po_kernel(tc, x_words, x_scales, w1, w2, gain, offs, out_0, out_1, out_2):
@@ -62,8 +63,8 @@ def tile_picked_ygem_none_po_kernel(tc, x_words, x_scales, w1, w2, gain, offs, o
         nc.scalar.activation(mean_bias[:], ones[:], ACT.Ln, scale=float(D) ** (-1.0 / 3.0))
 
         def deal(copy, grouped, raw, h, a, b):
-            dst = grouped[:].rearrange("p (t m j) -> p m t j", t=PACK, j=PACK)[:, 64 * h + a : 64 * h + b]
-            src = raw[:].rearrange("p j (m t) -> p m t j", t=PACK)[:, a:b]
+            dst = grouped[:].rearrange("p (t m j) -> p m j t", t=PACK, j=PACK)[:, 64 * h + a : 64 * h + b]
+            src = raw[:].rearrange("p j (m t) -> p m j t", t=PACK)[:, a:b]
             copy(dst, src)
 
         x_scale_tiles = []
@@ -258,7 +259,8 @@ def tile_picked_ygem_none_po_kernel(tc, x_words, x_scales, w1, w2, gain, offs, o
 
         def weave(copy, c, source):
             lo, hi = spans[c]
-            copy(res_bf[:, lo * PACK : hi * PACK].rearrange("p (v t) -> p v t", t=PACK), source.rearrange("p t v -> p v t"))
+            target = res_bf[:, lo * PACK : hi * PACK].rearrange("p (c i t) -> p c t i", t=PACK, i=LINE)
+            copy(target, source.rearrange("p t (c i) -> p c t i", i=LINE))
 
         split = spans[3][0]
         early_codes = keep.tile([P, split], U32, name="early_codes", align_bytes=64)

@@ -35,9 +35,6 @@ def tile_picked_ygem_none_po_kernel(tc, x_words, x_scales, w1, w2, gain, offs, o
         keep = ctx.enter_context(tc.tile_pool(name="keep", bufs=1))
         psum = ctx.enter_context(tc.psum_pool(name="psum", bufs=8))
 
-        offsets = keep.tile([P, S // 16], U16, name="offsets")
-        nc.sync.dma_start(offsets[:], offs)
-
         scale_table = keep.tile([P, T], U8, name="scale_table", align_bytes=64)
         nc.vector.memset(scale_table[:].bitcast(I32), 0)
 
@@ -47,6 +44,8 @@ def tile_picked_ygem_none_po_kernel(tc, x_words, x_scales, w1, w2, gain, offs, o
             return raw
 
         w1_raw = [load_half(w1, "w1", 0)]
+        offsets = keep.tile([P, S // 16], U16, name="offsets")
+        nc.sync.dma_start(offsets[:], offs)
         for q in range(4):
             nc.sync.dma_start(scale_table[32 * q : 32 * q + 4, :].bitcast(I32), x_scales[0, 4 * q : 4 * q + 4, :].bitcast(I32))
         w1_raw.append(load_half(w1, "w1", 1))
@@ -178,10 +177,10 @@ def tile_picked_ygem_none_po_kernel(tc, x_words, x_scales, w1, w2, gain, offs, o
         w2_bf = keep.tile([P, PACK * N], BF16, name="w2_bf", tag="cubes7", align_bytes=64)
         w2_codes = keep.tile([P, N], U32, name="w2_codes", align_bytes=64)
         w2_scales = keep.tile([P, N], U8, name="w2_scales", align_bytes=64)
-        w2_dst = w2_bf[:].rearrange("p (t m j) -> p m t j", t=PACK, j=PACK)
-        w2_src = w2_raw[:].rearrange("p j (m t) -> p m t j", t=PACK)
+        w2_dst = w2_bf[:].rearrange("p (t m j) -> p m j t", t=PACK, j=PACK)
+        w2_src = w2_raw[:].rearrange("p j (m t) -> p m j t", t=PACK)
         for u in range(2):
-            nc.vector.tensor_copy(w2_dst[:, :, 2 * u : 2 * u + 2], w2_src[:, :, 2 * u : 2 * u + 2])
+            nc.vector.tensor_copy(w2_dst[:, :, :, 2 * u : 2 * u + 2], w2_src[:, :, :, 2 * u : 2 * u + 2])
         for u in range(2):
             cols = slice(256 * u, 256 * (u + 1))
             nc.vector.quantize_mx(out=w2_codes[:, cols].bitcast(FP8X4), scales=w2_scales[:, cols], in_=w2_bf[:, 1024 * u : 1024 * (u + 1)])

@@ -87,7 +87,7 @@ def tile_picked_ygem_none_po_kernel(tc, x_words, x_scales, w1, w2, gain, offs, o
         sums = keep.tile([P, V * PACK], F32, name="sums", tag="pooled")
         logs = keep.tile([P, V * PACK], F32, name="logs")
         pieces = [(0, 2), (2, 4), (4, 6), (6, 7), (7, 8)]
-        sum_ranges = [(0, 2), (2, 4), (4, 5), (5, 6), (6, 7), (7, 8)]
+        sum_ranges = [(128, 256), (256, 320), (320, 384), (384, 448), (448, 480), (480, 512)]
         piece_of = {b: n for n, (lo, hi) in enumerate(pieces) for b in range(lo, hi)}
         cubes = {n: keep.tile([P, (hi - lo) * BJ, PACK], F32, name=f"cubes{lo}", tag=f"cubes{lo}", align_bytes=64) for n, (lo, hi) in enumerate(pieces) if n > 0}
         odds = {n: keep.tile([P, (hi - lo) * BJ // D, PACK], F32, name=f"odds{lo}") for n, (lo, hi) in enumerate(pieces) if n > 0}
@@ -136,11 +136,11 @@ def tile_picked_ygem_none_po_kernel(tc, x_words, x_scales, w1, w2, gain, offs, o
                 nc.vector.tensor_scalar(odds[n][:], pairs[:, :, 1, :], SHIFT**3, None, ALU.max)
 
         def pool_pairs(lo, hi):
-            n = piece_of[lo]
-            first = pieces[n][0]
-            images = slice((lo - first) * BJ // D, (hi - first) * BJ // D)
+            n = piece_of[lo * D // BJ]
+            first = pieces[n][0] * BJ // D
+            images = slice(lo - first, hi - first)
             pairs = cubes[n][:].rearrange("p (v e) t -> p v e t", e=D)
-            cols = slice(lo * BJ // D * PACK, hi * BJ // D * PACK)
+            cols = slice(lo * PACK, hi * PACK)
             total = sums[:, cols].rearrange("p (v t) -> p v t", t=PACK)
             nc.vector.scalar_tensor_tensor(total, pairs[:, images, 0, :], SHIFT**3, odds[n][:, images, :], ALU.max, ALU.add)
 
@@ -151,16 +151,16 @@ def tile_picked_ygem_none_po_kernel(tc, x_words, x_scales, w1, w2, gain, offs, o
         floor_odd(1)
         cube(4)
         cube(5)
-        pool_pairs(2, 4)
+        pool_pairs(*sum_ranges[0])
         floor_odd(2)
         cube(6)
         floor_odd(3)
         cube(7)
-        pool_pairs(4, 5)
-        pool_pairs(5, 6)
+        pool_pairs(*sum_ranges[1])
+        pool_pairs(*sum_ranges[2])
         floor_odd(4)
-        pool_pairs(6, 7)
-        pool_pairs(7, 8)
+        for images in sum_ranges[3:]:
+            pool_pairs(*images)
         turned_sums = psum.tile([P, PACK, P], F32, name="acc")
         for t in range(PACK):
             for e in range(D):
@@ -170,20 +170,24 @@ def tile_picked_ygem_none_po_kernel(tc, x_words, x_scales, w1, w2, gain, offs, o
         first_logs = psum.tile([P, PACK, P], F32, name="acc")
         for t in range(PACK):
             nc.tensor.transpose(first_logs[:, t, :], turned_logs[:, t, :], identity[:])
-        for lo, hi in sum_ranges[1:]:
-            cols = slice(lo * BJ // D * PACK, hi * BJ // D * PACK)
-            nc.scalar.activation(logs[:, cols], sums[:, cols], ACT.Ln, bias=SHIFT**3 if lo == 6 else 0.0)
+        for lo, hi in sum_ranges:
+            cols = slice(lo * PACK, hi * PACK)
+            nc.scalar.activation(logs[:, cols], sums[:, cols], ACT.Ln, bias=SHIFT**3 if lo == 384 else 0.0)
 
         w2_bf = keep.tile([P, PACK * N], BF16, name="w2_bf", tag="cubes7", align_bytes=64)
         w2_codes = keep.tile([P, N], U32, name="w2_codes", align_bytes=64)
         w2_scales = keep.tile([P, N], U8, name="w2_scales", align_bytes=64)
         w2_dst = w2_bf[:].rearrange("p (t m j) -> p m j t", t=PACK, j=PACK)
         w2_src = w2_raw[:].rearrange("p j (m t) -> p m j t", t=PACK)
-        for u in range(2):
-            nc.vector.tensor_copy(w2_dst[:, :, :, 2 * u : 2 * u + 2], w2_src[:, :, :, 2 * u : 2 * u + 2])
-        for u in range(2):
+
+        def quantise_w2(u):
             cols = slice(256 * u, 256 * (u + 1))
             nc.vector.quantize_mx(out=w2_codes[:, cols].bitcast(FP8X4), scales=w2_scales[:, cols], in_=w2_bf[:, 1024 * u : 1024 * (u + 1)])
+
+        nc.vector.tensor_copy(w2_dst[:, :, :, 0:2], w2_src[:, :, :, 0:2])
+        nc.vector.tensor_copy(w2_dst[:, :64, :, 2:4], w2_src[:, :64, :, 2:4])
+        quantise_w2(0)
+        nc.vector.tensor_copy(w2_dst[:, 64:, :, 2:4], w2_src[:, 64:, :, 2:4])
 
         idle = psum.tile([P, 512], F32, name="acc")
         for n in range(WARM_UPS):
@@ -203,7 +207,7 @@ def tile_picked_ygem_none_po_kernel(tc, x_words, x_scales, w1, w2, gain, offs, o
         out_words = out_1[0].rearrange("p c r -> p (c r)")
         edges = [0, 64, 192, 320, 448, 512]
         spans = list(zip(edges[:-1], edges[1:]))
-        z_all = keep.tile([P, V * PACK], BF16, name="z_all", tag="cubes7", align_bytes=64)
+        z_all = keep.tile([P, V * PACK], BF16, name="z_all", align_bytes=64)
         z_bf = [z_all[:, lo * PACK : hi * PACK] for lo, hi in spans]
         tail_lo = spans[3][0]
         res_tail = keep.tile([P, PACK, V - tail_lo], F32, name="res_tail")
@@ -213,16 +217,14 @@ def tile_picked_ygem_none_po_kernel(tc, x_words, x_scales, w1, w2, gain, offs, o
 
         last = len(spans) - 1
 
-        def root(c):
-            lo, hi = spans[c]
+        def root(lo, hi):
+            cols = slice(lo * PACK, hi * PACK)
             if lo < P:
-                top = min(hi, P)
-                woven = first_logs[:].rearrange("p t v -> p v t")[:, lo:top]
-                nc.scalar.activation(roots[:, lo * PACK : top * PACK].rearrange("p (v t) -> p v t", t=PACK), woven, ACT.Exp, bias=mean_bias[:], scale=1.0 / 3.0)
-                lo = top
-            if lo < hi:
-                cols = slice(lo * PACK, hi * PACK)
-                nc.scalar.activation(roots[:, cols], logs[:, cols], ACT.Exp, bias=mean_bias[:], scale=1.0 / 3.0)
+                source = first_logs[:].rearrange("p t v -> p v t")[:, lo:hi]
+                target = roots[:, cols].rearrange("p (v t) -> p v t", t=PACK)
+            else:
+                source, target = logs[:, cols], roots[:, cols]
+            nc.scalar.activation(target, source, ACT.Exp, bias=mean_bias[:], scale=1.0 / 3.0)
 
         def apply_gain(lo, hi):
             cols = slice(lo * PACK, hi * PACK)
@@ -274,9 +276,11 @@ def tile_picked_ygem_none_po_kernel(tc, x_words, x_scales, w1, w2, gain, offs, o
             if c in (2, 3):
                 nc.sync.dma_start(out_words[:, first * PACK : (first + codes.shape[1]) * PACK].bitcast(I32), codes[:].bitcast(I32))
 
-        for c in range(len(spans)):
-            root(c)
-        apply_gain(0, 64)
+        for lo, hi in [(0, 32), (32, 64), (64, 128), (128, 192)] + spans[2:]:
+            root(lo, hi)
+        apply_gain(0, 32)
+        apply_gain(32, 64)
+        quantise_w2(1)
         whiten(0)
         apply_gain(64, 192)
         for c in range(1, last):

@@ -180,14 +180,16 @@ def tile_picked_ygem_none_po_kernel(tc, x_words, x_scales, w1, w2, gain, offs, o
         w2_dst = w2_bf[:].rearrange("p (t m j) -> p m j t", t=PACK, j=PACK)
         w2_src = w2_raw[:].rearrange("p j (m t) -> p m j t", t=PACK)
 
-        def quantise_w2(u):
-            cols = slice(256 * u, 256 * (u + 1))
-            nc.vector.quantize_mx(out=w2_codes[:, cols].bitcast(FP8X4), scales=w2_scales[:, cols], in_=w2_bf[:, 1024 * u : 1024 * (u + 1)])
+        def quantise_w2(lo, hi):
+            nc.vector.quantize_mx(out=w2_codes[:, lo:hi].bitcast(FP8X4), scales=w2_scales[:, lo:hi], in_=w2_bf[:, lo * PACK : hi * PACK])
 
         nc.vector.tensor_copy(w2_dst[:, :, :, 0:2], w2_src[:, :, :, 0:2])
         nc.vector.tensor_copy(w2_dst[:, :64, :, 2:4], w2_src[:, :64, :, 2:4])
-        quantise_w2(0)
+        quantise_w2(0, 2 * P)
         nc.vector.tensor_copy(w2_dst[:, 64:, :, 2:4], w2_src[:, 64:, :, 2:4])
+        for half in range(2):
+            for t in (2, 3):
+                quantise_w2(t * P + 64 * half, t * P + 64 * (half + 1))
 
         idle = psum.tile([P, 512], F32, name="acc")
         for n in range(WARM_UPS):
@@ -276,17 +278,15 @@ def tile_picked_ygem_none_po_kernel(tc, x_words, x_scales, w1, w2, gain, offs, o
             if c in (2, 3):
                 nc.sync.dma_start(out_words[:, first * PACK : (first + codes.shape[1]) * PACK].bitcast(I32), codes[:].bitcast(I32))
 
-        for lo, hi in [(0, 32), (32, 64), (64, 128), (128, 192)] + spans[2:]:
+        for lo, hi in [(0, 32), (32, 64)] + [(lo, lo + 64) for lo in range(64, 320, 64)] + spans[3:]:
             root(lo, hi)
         apply_gain(0, 32)
         apply_gain(32, 64)
-        quantise_w2(1)
+        apply_gain(64, 128)
         whiten(0)
-        apply_gain(64, 192)
         for c in range(1, last):
             hi = spans[c][1]
-            if c > 1:
-                apply_gain(hi - 64, hi)
+            apply_gain(hi - 64, hi)
             apply_gain(hi, hi + 64)
             whiten(c)
         whiten(last)

@@ -25,7 +25,6 @@ CHUNKS = 4
 CV = V // CHUNKS
 CJ = CV * D
 BJ = 128
-WARM_UPS = 3
 LINE = 4
 
 
@@ -190,18 +189,6 @@ def tile_picked_ygem_none_po_kernel(tc, x_words, x_scales, w1, w2, gain, offs, o
         for half in range(2):
             for t in (2, 3):
                 quantise_w2(t * P + 64 * half, t * P + 64 * (half + 1))
-
-        idle = psum.tile([P, 512], F32, name="acc")
-        for n in range(WARM_UPS):
-            nc.tensor.matmul_mx(
-                out=idle[:],
-                lhsT=w2_codes[:, 0:P].bitcast(FP8X4),
-                lhsT_scale=w2_scales[:, 0:P],
-                rhs=w1_codes[:].bitcast(FP8X4),
-                rhs_scale=w1_scales[:],
-                start=True,
-                stop=True,
-            )
 
         roots = keep.tile([P, V * PACK], F32, name="roots", tag="pooled")
         out_scales = keep.tile([P, V], U8, name="out_scales", align_bytes=64)

@@ -25,6 +25,7 @@ CHUNKS = 4
 CV = V // CHUNKS
 CJ = CV * D
 BJ = 128
+WARM_UP_COLUMNS = (512, 64)
 LINE = 4
 
 
@@ -189,6 +190,18 @@ def tile_picked_ygem_none_po_kernel(tc, x_words, x_scales, w1, w2, gain, offs, o
         for half in range(2):
             for t in (2, 3):
                 quantise_w2(t * P + 64 * half, t * P + 64 * (half + 1))
+
+        idle = psum.tile([P, 512], F32, name="acc")
+        for width in WARM_UP_COLUMNS:
+            nc.tensor.matmul_mx(
+                out=idle[:, :width],
+                lhsT=w2_codes[:, N - P :].bitcast(FP8X4),
+                lhsT_scale=w2_scales[:, N - P :],
+                rhs=w1_codes[:, :width].bitcast(FP8X4),
+                rhs_scale=w1_scales[:, :width],
+                start=True,
+                stop=True,
+            )
 
         roots = keep.tile([P, V * PACK], F32, name="roots", tag="pooled")
         out_scales = keep.tile([P, V], U8, name="out_scales", align_bytes=64)

@@ -66,11 +66,8 @@ def tile_picked_ygem_none_po_kernel(tc, x_words, x_scales, w1, w2, gain, offs, o
             src = raw[:].rearrange("p j (m t) -> p m j t", t=PACK)[:, a:b]
             copy(dst, src)
 
-        x_scale_tiles = []
-        for g in range(2):
-            xs = keep.tile([P, 512], U8, name=f"xs{g}", align_bytes=64)
-            nc.vector.tensor_copy(xs[:], scale_table[:].indirect(offsets[:, 32 * g : 32 * (g + 1)]))
-            x_scale_tiles.append(xs)
+        picked_scales = keep.tile([P, S], U8, name="picked_scales", align_bytes=64)
+        nc.vector.tensor_copy(picked_scales[:], scale_table[:].indirect(offsets[:]))
         w1_bf = keep.tile([P, PACK * H], BF16, name="w1_bf", align_bytes=64)
         deal(nc.scalar.copy, w1_bf, w1_raw[0], 0, 0, 64)
         deal(nc.scalar.copy, w1_bf, w1_raw[1], 1, 0, 64)
@@ -89,17 +86,16 @@ def tile_picked_ygem_none_po_kernel(tc, x_words, x_scales, w1, w2, gain, offs, o
         pieces = [(0, 2), (2, 4), (4, 6), (6, 7), (7, 8)]
         sum_ranges = [(128, 256), (256, 320), (320, 384), (384, 448), (448, 480), (480, 512)]
         piece_of = {b: n for n, (lo, hi) in enumerate(pieces) for b in range(lo, hi)}
-        cubes = {n: keep.tile([P, (hi - lo) * BJ, PACK], F32, name=f"cubes{lo}", tag=f"cubes{lo}", align_bytes=64) for n, (lo, hi) in enumerate(pieces) if n > 0}
+        cubes = {n: keep.tile([P, (hi - lo) * BJ, PACK], F32, name=f"cubes{lo}", tag=f"cubes{lo}", align_bytes=64) for n, (lo, hi) in enumerate(pieces)}
         odds = {n: keep.tile([P, (hi - lo) * BJ // D, PACK], F32, name=f"odds{lo}") for n, (lo, hi) in enumerate(pieces) if n > 0}
 
-        parted_cubes = keep.tile([P, D, PACK, P], F32, name="parted_cubes")
-        floored = keep.tile([P, D, PACK, P], F32, name="floored")
+        floored = keep.tile([P, D, P, PACK], F32, name="floored")
         identity = keep.tile([P, P], F32, name="identity")
         make_identity(nc, identity[:])
 
         def cube(b):
             acc = psum.tile([P, PACK, BJ], F32, name="acc")
-            xs = x_scale_tiles[b // 4][:, (b % 4) * BJ : (b % 4 + 1) * BJ]
+            xs = picked_scales[:, b * BJ : (b + 1) * BJ]
             xc = x_code_tiles[b]
             for t in range(PACK):
                 nc.tensor.matmul_mx(
@@ -111,20 +107,17 @@ def tile_picked_ygem_none_po_kernel(tc, x_words, x_scales, w1, w2, gain, offs, o
                     start=True,
                     stop=True,
                 )
-            if b < 2:
-                parted = acc[:].rearrange("p t (v e) -> p e t v", e=D)
-                sq = keep.tile([P, D, PACK, BJ // D], F32, name=f"sq{b}")
-                nc.scalar.activation(sq[:], parted, ACT.Square, bias=SHIFT)
-                images = slice(b * BJ // D, (b + 1) * BJ // D)
-                nc.vector.scalar_tensor_tensor(parted_cubes[:, :, :, images], parted, SHIFT, sq[:], ALU.add, ALU.mult)
-                nc.gpsimd.tensor_scalar(floored[:, :, :, images], parted_cubes[:, :, :, images], F32_MAX, SHIFT**3, ALU.min, ALU.max)
-                return
             woven = acc[:].rearrange("p t j -> p j t")
             sq = keep.tile([P, BJ, PACK], F32, name=f"sq{b}")
             nc.scalar.activation(sq[:], woven, ACT.Square, bias=SHIFT)
             n = piece_of[b]
             at = (b - pieces[n][0]) * BJ
             nc.vector.scalar_tensor_tensor(cubes[n][:, at : at + BJ, :], woven, SHIFT, sq[:], ALU.add, ALU.mult)
+
+        def floor_both(b):
+            images = slice(b * BJ // D, (b + 1) * BJ // D)
+            pairs = cubes[0][:].rearrange("p (v e) t -> p e v t", e=D)
+            nc.gpsimd.tensor_scalar(floored[:, :, images], pairs[:, :, images], F32_MAX, SHIFT**3, ALU.min, ALU.max)
 
         def floor_odd(n):
             pairs = cubes[n][:].rearrange("p (v e) t -> p v e t", e=D)
@@ -145,7 +138,9 @@ def tile_picked_ygem_none_po_kernel(tc, x_words, x_scales, w1, w2, gain, offs, o
             nc.vector.scalar_tensor_tensor(total, pairs[:, images, 0, :], SHIFT**3, odds[n][:, images, :], ALU.max, ALU.add)
 
         cube(0)
+        floor_both(0)
         cube(1)
+        floor_both(1)
         cube(2)
         cube(3)
         floor_odd(1)
@@ -162,9 +157,10 @@ def tile_picked_ygem_none_po_kernel(tc, x_words, x_scales, w1, w2, gain, offs, o
         for images in sum_ranges[3:]:
             pool_pairs(*images)
         turned_sums = psum.tile([P, PACK, P], F32, name="acc")
-        for t in range(PACK):
+        for g in range(PACK):
             for e in range(D):
-                nc.tensor.matmul(turned_sums[:, t, :], floored[:, e, t, :], identity[:], start=e == 0, stop=e == D - 1, is_transpose=True)
+                group = floored[:, e, 32 * g : 32 * (g + 1), :].rearrange("p v t -> p (v t)")
+                nc.tensor.matmul(turned_sums[:, g, :], group, identity[:], start=e == 0, stop=e == D - 1, is_transpose=True)
         turned_logs = keep.tile([P, PACK, P], F32, name="turned_logs")
         nc.scalar.activation(turned_logs[:], turned_sums[:], ACT.Ln)
         first_logs = psum.tile([P, PACK, P], F32, name="acc")
@@ -221,12 +217,8 @@ def tile_picked_ygem_none_po_kernel(tc, x_words, x_scales, w1, w2, gain, offs, o
 
         def root(lo, hi):
             cols = slice(lo * PACK, hi * PACK)
-            if lo < P:
-                source = first_logs[:].rearrange("p t v -> p v t")[:, lo:hi]
-                target = roots[:, cols].rearrange("p (v t) -> p v t", t=PACK)
-            else:
-                source, target = logs[:, cols], roots[:, cols]
-            nc.scalar.activation(target, source, ACT.Exp, bias=mean_bias[:], scale=1.0 / 3.0)
+            source = first_logs[:].rearrange("p g c -> p (g c)") if lo < P else logs[:]
+            nc.scalar.activation(roots[:, cols], source[:, cols], ACT.Exp, bias=mean_bias[:], scale=1.0 / 3.0)
 
         def apply_gain(lo, hi):
             cols = slice(lo * PACK, hi * PACK)

@@ -203,10 +203,9 @@ def tile_picked_ygem_none_po_kernel(tc, x_words, x_scales, w1, w2, gain, offs, o
         out_scales = keep.tile([P, V], U8, name="out_scales", align_bytes=64)
         out_rows = out_0.rearrange("(p t) v -> p t v", t=PACK)
         out_words = out_1[0].rearrange("p c r -> p (c r)")
-        edges = [0, 64, 192, 320, 448, 512]
+        edges = [0, 128, 256, 384, 448, 512]
         spans = list(zip(edges[:-1], edges[1:]))
         z_all = keep.tile([P, V * PACK], BF16, name="z_all", align_bytes=64)
-        z_bf = [z_all[:, lo * PACK : hi * PACK] for lo, hi in spans]
         tail_lo = spans[3][0]
         res_tail = keep.tile([P, PACK, V - tail_lo], F32, name="res_tail")
         res = [keep.tile([P, PACK, hi - lo], F32, name=f"res{lo}")[:] for lo, hi in spans[:3]]
@@ -229,28 +228,32 @@ def tile_picked_ygem_none_po_kernel(tc, x_words, x_scales, w1, w2, gain, offs, o
                 ALU.mult,
             )
 
-        def whiten(c):
-            lo, hi = spans[c]
-            zc = keep.tile([P, hi - lo], U32, name=f"zc{c}", align_bytes=64)
-            zs = keep.tile([P, hi - lo], U8, name=f"zs{c}", align_bytes=64)
-            nc.vector.quantize_mx(out=zc[:].bitcast(FP8X4), scales=zs[:], in_=z_bf[c])
-            acc = psum.tile([P, PACK, hi - lo], F32, name="acc")
-            for t in range(PACK):
-                nc.tensor.matmul_mx(
-                    out=acc[:, t, :],
-                    lhsT=w2_codes[:, t * P : (t + 1) * P].bitcast(FP8X4),
-                    lhsT_scale=w2_scales[:, t * P : (t + 1) * P],
-                    rhs=zc[:].bitcast(FP8X4),
-                    rhs_scale=zs[:],
-                    start=True,
-                    stop=True,
-                )
-            nc.scalar.copy(res[c], acc[:])
-            if c < 3:
-                nc.sync.dma_start(out_rows[:, :, lo:hi], res[c])
-            if c == last:
+        def whiten(lo, hi):
+            zc = keep.tile([P, hi - lo], U32, name=f"zc{lo}", align_bytes=64)
+            zs = keep.tile([P, hi - lo], U8, name=f"zs{lo}", align_bytes=64)
+            nc.vector.quantize_mx(out=zc[:].bitcast(FP8X4), scales=zs[:], in_=z_all[:, lo * PACK : hi * PACK])
+            per_bank = 2 if lo == 0 else PACK
+            for first in range(0, PACK, per_bank):
+                acc = psum.tile([P, per_bank, hi - lo], F32, name="acc")
+                for t in range(first, first + per_bank):
+                    nc.tensor.matmul_mx(
+                        out=acc[:, t - first, :],
+                        lhsT=w2_codes[:, t * P : (t + 1) * P].bitcast(FP8X4),
+                        lhsT_scale=w2_scales[:, t * P : (t + 1) * P],
+                        rhs=zc[:].bitcast(FP8X4),
+                        rhs_scale=zs[:],
+                        start=True,
+                        stop=True,
+                    )
+                if hi < V:
+                    nc.scalar.copy(res[lo // P][:, first : first + per_bank], acc[:])
+            if hi < V:
+                nc.sync.dma_start(out_rows[:, :, lo:hi], res[lo // P])
+            else:
+                for c in (last - 1, last):
+                    nc.scalar.copy(res[c], acc[:, :, spans[c][0] - lo : spans[c][1] - lo])
                 nc.sync.dma_start(out_rows[:, :, tail_lo:V], res_tail[:])
-                weave(nc.scalar.copy, c, acc[:])
+                weave(nc.scalar.copy, last, acc[:, :, spans[last][0] - lo :])
 
         def weave(copy, c, source):
             lo, hi = spans[c]
@@ -270,18 +273,14 @@ def tile_picked_ygem_none_po_kernel(tc, x_words, x_scales, w1, w2, gain, offs, o
             if c in (2, 3):
                 nc.sync.dma_start(out_words[:, first * PACK : (first + codes.shape[1]) * PACK].bitcast(I32), codes[:].bitcast(I32))
 
-        for lo, hi in [(0, 32), (32, 64)] + [(lo, lo + 64) for lo in range(64, 320, 64)] + spans[3:]:
+        pieces_of_roots = [(0, 32), (32, 64)] + [(lo, lo + 64) for lo in range(64, V, 64)]
+        for lo, hi in pieces_of_roots:
             root(lo, hi)
-        apply_gain(0, 32)
-        apply_gain(32, 64)
-        apply_gain(64, 128)
-        whiten(0)
-        for c in range(1, last):
-            hi = spans[c][1]
-            apply_gain(hi - 64, hi)
-            apply_gain(hi, hi + 64)
-            whiten(c)
-        whiten(last)
+        for lo, hi in pieces_of_roots:
+            apply_gain(lo, hi)
+            if lo > 0 and lo % P == 0:
+                whiten(lo - P, lo)
+        whiten(V - P, V)
         for c in range(last):
             weave(nc.vector.tensor_copy, c, res[c])
             if c > 0:

@@ -27,13 +27,20 @@ CJ = CV * D
 BJ = 128
 WARM_UP_COLUMNS = (512, 64)
 LINE = 4
+TURNED = 10
+BANKS = S // BJ
+TURN = P // PACK
+SPANS = V // P
 
 
 def tile_picked_ygem_none_po_kernel(tc, x_words, x_scales, w1, w2, gain, offs, out_0, out_1, out_2):
     nc = tc.nc
     with ExitStack() as ctx:
         keep = ctx.enter_context(tc.tile_pool(name="keep", bufs=1))
-        psum = ctx.enter_context(tc.psum_pool(name="psum", bufs=8))
+        psum = ctx.enter_context(tc.psum_pool(name="psum", bufs=1))
+
+        def bank(n, name):
+            return psum.tile([P, PACK, P], F32, name=name, tag=f"bank{n}")
 
         scale_table = keep.tile([P, T], U8, name="scale_table", align_bytes=64)
         nc.vector.memset(scale_table[:].bitcast(I32), 0)
@@ -76,99 +83,106 @@ def tile_picked_ygem_none_po_kernel(tc, x_words, x_scales, w1, w2, gain, offs, o
         nc.vector.quantize_mx(out=w1_codes[:].bitcast(FP8X4), scales=w1_scales[:], in_=w1_bf[:])
 
         x_code_tiles = []
-        for lo, hi in [(0, 256), (256, 512), (512, 1024)]:
+        for lo, hi in [(0, 128), (128, 384), (384, 1024)]:
             xc = keep.tile([P, hi - lo], U32, name=f"xc{lo}", align_bytes=64)
             nc.vector.tensor_copy(xc[:], word_table[:].indirect(offsets[:, lo // 16 : hi // 16]))
             x_code_tiles.extend(xc[:, at : at + BJ] for at in range(0, hi - lo, BJ))
 
-        sums = keep.tile([P, V * PACK], F32, name="sums", tag="pooled")
-        logs = keep.tile([P, V * PACK], F32, name="logs")
-        pieces = [(0, 2), (2, 4), (4, 6), (6, 7), (7, 8)]
-        sum_ranges = [(128, 256), (256, 320), (320, 384), (384, 448), (448, 480), (480, 512)]
-        piece_of = {b: n for n, (lo, hi) in enumerate(pieces) for b in range(lo, hi)}
-        cubes = {n: keep.tile([P, (hi - lo) * BJ, PACK], F32, name=f"cubes{lo}", tag=f"cubes{lo}", align_bytes=64) for n, (lo, hi) in enumerate(pieces)}
-        odds = {n: keep.tile([P, (hi - lo) * BJ // D, PACK], F32, name=f"odds{lo}") for n, (lo, hi) in enumerate(pieces) if n > 0}
-
-        floored = keep.tile([P, D, P, PACK], F32, name="floored")
         identity = keep.tile([P, P], F32, name="identity")
         make_identity(nc, identity[:])
+        pieces = [(0, 1), (1, 3), (3, 4), (4, 5), (5, 6), (6, 7), (7, 8)]
+        cube_tiles = {lo: keep.tile([P, (hi - lo) * BJ, PACK], F32, name=f"cubes{lo}", tag=f"cubes{lo}", align_bytes=64) for lo, hi in pieces}
+        cubes = [cube_tiles[lo][:, (b - lo) * BJ : (b - lo + 1) * BJ] for lo, hi in pieces for b in range(lo, hi)]
+        floored = {}
+        turned_logs = keep.tile([P, TURNED * P], F32, name="turned_logs")
 
         def cube(b):
-            acc = psum.tile([P, PACK, BJ], F32, name="acc")
-            xs = picked_scales[:, b * BJ : (b + 1) * BJ]
-            xc = x_code_tiles[b]
+            acc = bank(b, f"acc{b}")
             for t in range(PACK):
                 nc.tensor.matmul_mx(
                     out=acc[:, t, :],
                     lhsT=w1_codes[:, t * P : (t + 1) * P].bitcast(FP8X4),
                     lhsT_scale=w1_scales[:, t * P : (t + 1) * P],
-                    rhs=xc.bitcast(FP8X4),
-                    rhs_scale=xs,
+                    rhs=x_code_tiles[b].bitcast(FP8X4),
+                    rhs_scale=picked_scales[:, b * BJ : (b + 1) * BJ],
                     start=True,
                     stop=True,
                 )
             woven = acc[:].rearrange("p t j -> p j t")
-            sq = keep.tile([P, BJ, PACK], F32, name=f"sq{b}")
+            sq = keep.tile([P, BJ, PACK], F32, name=f"sq{b}", tag=f"sq{b}" if b < BANKS - 1 else "pooled", align_bytes=64)
             nc.scalar.activation(sq[:], woven, ACT.Square, bias=SHIFT)
-            n = piece_of[b]
-            at = (b - pieces[n][0]) * BJ
-            nc.vector.scalar_tensor_tensor(cubes[n][:, at : at + BJ, :], woven, SHIFT, sq[:], ALU.add, ALU.mult)
+            nc.vector.scalar_tensor_tensor(cubes[b], woven, SHIFT, sq[:], ALU.add, ALU.mult)
 
-        def floor_both(b):
-            images = slice(b * BJ // D, (b + 1) * BJ // D)
-            pairs = cubes[0][:].rearrange("p (v e) t -> p e v t", e=D)
-            nc.gpsimd.tensor_scalar(floored[:, :, images], pairs[:, :, images], F32_MAX, SHIFT**3, ALU.min, ALU.max)
+        def floor(lo, hi, tile):
+            pairs = cube_tiles[lo // 2][:].rearrange("p (v e) t -> p e v t", e=D)
+            for a in range(lo, hi):
+                floored[a] = tile[:, :, (a - lo) * TURN : (a - lo + 1) * TURN]
+            nc.gpsimd.tensor_scalar(tile, pairs, F32_MAX, SHIFT**3, ALU.min, ALU.max)
 
-        def floor_odd(n):
-            pairs = cubes[n][:].rearrange("p (v e) t -> p v e t", e=D)
-            if n == 3:
-                nc.scalar.activation(odds[n][:], pairs[:, :, 1, :], ACT.Relu, bias=-(SHIFT**3))
-            elif n < 3:
-                nc.gpsimd.tensor_scalar(odds[n][:], pairs[:, :, 1, :], F32_MAX, SHIFT**3, ALU.min, ALU.max)
+        def floored_tile(lo, hi, tag):
+            return keep.tile([P, D, (hi - lo) * TURN, PACK], F32, name=f"floored{lo}", tag=tag, align_bytes=64)[:]
+
+        def pool_pairs(lo, hi, n, bias=0.0):
+            sums = bank(n, f"sums{lo}")
+            for a in range(lo, hi):
+                for e in range(D):
+                    group = floored[a][:, e].rearrange("p v t -> p (v t)")
+                    nc.tensor.matmul(sums[:, a - lo, :], group, identity[:], start=e == 0, stop=e == D - 1, is_transpose=True)
+            nc.scalar.activation(turned_logs[:, lo * P : hi * P], sums[:, : hi - lo, :].rearrange("p a c -> p (a c)"), ACT.Ln, bias=bias)
+
+        logs = []
+
+        def turn_back(g):
+            logs.append(bank(3 + g, f"logs{g}"))
+            for a in range(min(PACK, TURNED - g * PACK)):
+                at = (g * PACK + a) * P
+                nc.tensor.transpose(logs[g][:, a, :] if at else first_logs, turned_logs[:, at : at + P], identity[:])
+
+        for b in range(BANKS):
+            cube(b)
+            if b in (0, 2, 3, 4):
+                lo, hi = 2 if b == 2 else 2 * b, 2 * b + 2
+                floor(lo, hi, floored_tile(lo, hi, f"floored{b}"))
+        first_plain = TURNED * TURN
+        scalar_odds = keep.tile([P, BJ // D, PACK], F32, name="scalar_odds")
+        late = keep.tile([P, 5, BJ // D, PACK], F32, name="late", tag="pooled", align_bytes=64)
+        odds = {5: scalar_odds[:], 6: late[:, 0], 7: late[:, 1]}
+        sums = late[:, 2:].rearrange("p b v t -> p (b v) t")
+        plain_logs = keep.tile([P, (V - first_plain) * PACK], F32, name="plain_logs")
+
+        def floor_odd(b):
+            pairs = cubes[b].rearrange("p (v e) t -> p v e t", e=D)
+            if b == 5:
+                nc.scalar.activation(odds[b], pairs[:, :, 1, :], ACT.Relu, bias=-(SHIFT**3))
             else:
-                nc.vector.tensor_scalar(odds[n][:], pairs[:, :, 1, :], SHIFT**3, None, ALU.max)
+                nc.vector.tensor_scalar(odds[b], pairs[:, :, 1, :], SHIFT**3, None, ALU.max)
 
-        def pool_pairs(lo, hi):
-            n = piece_of[lo * D // BJ]
-            first = pieces[n][0] * BJ // D
-            images = slice(lo - first, hi - first)
-            pairs = cubes[n][:].rearrange("p (v e) t -> p v e t", e=D)
-            cols = slice(lo * PACK, hi * PACK)
-            total = sums[:, cols].rearrange("p (v t) -> p v t", t=PACK)
-            nc.vector.scalar_tensor_tensor(total, pairs[:, images, 0, :], SHIFT**3, odds[n][:, images, :], ALU.max, ALU.add)
+        def add_plain(lo, hi):
+            b, at = divmod(lo, BJ // D)
+            pairs = cubes[b].rearrange("p (v e) t -> p v e t", e=D)[:, at : at + hi - lo]
+            images = slice(lo - first_plain, hi - first_plain)
+            nc.vector.scalar_tensor_tensor(sums[:, images], pairs[:, :, 0, :], SHIFT**3, odds[b][:, at : at + hi - lo], ALU.max, ALU.add)
 
-        cube(0)
-        floor_both(0)
-        cube(1)
-        floor_both(1)
-        cube(2)
-        cube(3)
-        floor_odd(1)
-        cube(4)
-        cube(5)
-        pool_pairs(*sum_ranges[0])
-        floor_odd(2)
-        cube(6)
-        floor_odd(3)
-        cube(7)
-        pool_pairs(*sum_ranges[1])
-        pool_pairs(*sum_ranges[2])
-        floor_odd(4)
-        for images in sum_ranges[3:]:
-            pool_pairs(*images)
-        turned_sums = psum.tile([P, PACK, P], F32, name="acc")
-        for g in range(PACK):
-            for e in range(D):
-                group = floored[:, e, 32 * g : 32 * (g + 1), :].rearrange("p v t -> p (v t)")
-                nc.tensor.matmul(turned_sums[:, g, :], group, identity[:], start=e == 0, stop=e == D - 1, is_transpose=True)
-        turned_logs = keep.tile([P, PACK, P], F32, name="turned_logs")
-        nc.scalar.activation(turned_logs[:], turned_sums[:], ACT.Ln)
-        first_logs = psum.tile([P, PACK, P], F32, name="acc")
-        for t in range(PACK):
-            nc.tensor.transpose(first_logs[:, t, :], turned_logs[:, t, :], identity[:])
-        for lo, hi in sum_ranges:
-            cols = slice(lo * PACK, hi * PACK)
-            nc.scalar.activation(logs[:, cols], sums[:, cols], ACT.Ln, bias=SHIFT**3 if lo == 384 else 0.0)
+        def plain_log(lo, hi):
+            images = slice(lo - first_plain, hi - first_plain)
+            nc.scalar.activation(plain_logs[:, images.start * PACK : images.stop * PACK], sums[:, images].rearrange("p v t -> p (v t)"), ACT.Ln, bias=SHIFT**3 if lo == first_plain else 0.0)
+
+        plain_ranges = [(320, 384), (384, 448), (448, 480), (480, 512)]
+        pool_pairs(0, 2, 0)
+        floor_odd(5)
+        floor_odd(6)
+        floor_odd(7)
+        for images in plain_ranges:
+            add_plain(*images)
+        pool_pairs(2, 6, 1)
+        pool_pairs(6, 8, 2)
+        plain_log(*plain_ranges[0])
+        pool_pairs(8, 10, 0)
+        for images in plain_ranges[1:]:
+            plain_log(*images)
+        first_logs = bank(7, "first_logs")[:, 0, :]
+        for g in range(3):
+            turn_back(g)
 
         w2_bf = keep.tile([P, PACK * N], BF16, name="w2_bf", tag="cubes7", align_bytes=64)
         w2_codes = keep.tile([P, N], U32, name="w2_codes", align_bytes=64)
@@ -187,7 +201,7 @@ def tile_picked_ygem_none_po_kernel(tc, x_words, x_scales, w1, w2, gain, offs, o
             for t in (2, 3):
                 quantise_w2(t * P + 64 * half, t * P + 64 * (half + 1))
 
-        idle = psum.tile([P, 512], F32, name="acc")
+        idle = bank(7, "idle")[:].rearrange("p a c -> p (a c)")
         for width in WARM_UP_COLUMNS:
             nc.tensor.matmul_mx(
                 out=idle[:, :width],
@@ -199,7 +213,7 @@ def tile_picked_ygem_none_po_kernel(tc, x_words, x_scales, w1, w2, gain, offs, o
                 stop=True,
             )
 
-        roots = keep.tile([P, V * PACK], F32, name="roots", tag="pooled")
+        roots = keep.tile([P, V * PACK], F32, name="roots", tag="pooled", align_bytes=64)
         out_scales = keep.tile([P, V], U8, name="out_scales", align_bytes=64)
         out_rows = out_0.rearrange("(p t) v -> p t v", t=PACK)
         out_words = out_1[0].rearrange("p c r -> p (c r)")
@@ -216,8 +230,13 @@ def tile_picked_ygem_none_po_kernel(tc, x_words, x_scales, w1, w2, gain, offs, o
 
         def root(lo, hi):
             cols = slice(lo * PACK, hi * PACK)
-            source = first_logs[:].rearrange("p g c -> p (g c)") if lo < P else logs[:]
-            nc.scalar.activation(roots[:, cols], source[:, cols], ACT.Exp, bias=mean_bias[:], scale=1.0 / 3.0)
+            if lo == 0:
+                source = first_logs
+            elif lo < first_plain:
+                source = logs[lo // P][:].rearrange("p g c -> p (g c)")[:, lo % P * PACK : (lo % P + hi - lo) * PACK]
+            else:
+                source = plain_logs[:, (lo - first_plain) * PACK : (hi - first_plain) * PACK]
+            nc.scalar.activation(roots[:, cols], source, ACT.Exp, bias=mean_bias[:], scale=1.0 / 3.0)
 
         def apply_gain(lo, hi):
             cols = slice(lo * PACK, hi * PACK)
@@ -234,7 +253,7 @@ def tile_picked_ygem_none_po_kernel(tc, x_words, x_scales, w1, w2, gain, offs, o
             nc.vector.quantize_mx(out=zc[:].bitcast(FP8X4), scales=zs[:], in_=z_all[:, lo * PACK : hi * PACK])
             per_bank = 2 if lo == 0 else PACK
             for first in range(0, PACK, per_bank):
-                acc = psum.tile([P, per_bank, hi - lo], F32, name="acc")
+                acc = bank((0, 1, 2, 6, 7)[lo // P + (lo + first > 0)], f"product{lo}")[:, :per_bank, :]
                 for t in range(first, first + per_bank):
                     nc.tensor.matmul_mx(
                         out=acc[:, t - first, :],
@@ -246,7 +265,7 @@ def tile_picked_ygem_none_po_kernel(tc, x_words, x_scales, w1, w2, gain, offs, o
                         stop=True,
                     )
                 if hi < V:
-                    nc.scalar.copy(res[lo // P][:, first : first + per_bank], acc[:])
+                    nc.scalar.copy(res[lo // P][:, first : first + per_bank], acc)
             if hi < V:
                 nc.sync.dma_start(out_rows[:, :, lo:hi], res[lo // P])
             else:

@@ -144,15 +144,15 @@ def tile_picked_ygem_none_po_kernel(tc, x_words, x_scales, w1, w2, gain, offs, o
                 lo, hi = 2 if b == 2 else 2 * b, 2 * b + 2
                 floor(lo, hi, floored_tile(lo, hi, f"floored{b}"))
         first_plain = TURNED * TURN
-        scalar_odds = keep.tile([P, BJ // D, PACK], F32, name="scalar_odds")
-        late = keep.tile([P, 5, BJ // D, PACK], F32, name="late", tag="pooled", align_bytes=64)
-        odds = {5: scalar_odds[:], 6: late[:, 0], 7: late[:, 1]}
-        sums = late[:, 2:].rearrange("p b v t -> p (b v) t")
+        scalar_odds = keep.tile([P, 2, BJ // D, PACK], F32, name="scalar_odds")
+        late = keep.tile([P, 4, BJ // D, PACK], F32, name="late", tag="pooled", align_bytes=64)
+        odds = {5: scalar_odds[:, 0], 6: scalar_odds[:, 1], 7: late[:, 0]}
+        sums = late[:, 1:].rearrange("p b v t -> p (b v) t")
         plain_logs = keep.tile([P, (V - first_plain) * PACK], F32, name="plain_logs")
 
         def floor_odd(b):
             pairs = cubes[b].rearrange("p (v e) t -> p v e t", e=D)
-            if b == 5:
+            if b < BANKS - 1:
                 nc.scalar.activation(odds[b], pairs[:, :, 1, :], ACT.Relu, bias=-(SHIFT**3))
             else:
                 nc.vector.tensor_scalar(odds[b], pairs[:, :, 1, :], SHIFT**3, None, ALU.max)
@@ -165,19 +165,19 @@ def tile_picked_ygem_none_po_kernel(tc, x_words, x_scales, w1, w2, gain, offs, o
 
         def plain_log(lo, hi):
             images = slice(lo - first_plain, hi - first_plain)
-            nc.scalar.activation(plain_logs[:, images.start * PACK : images.stop * PACK], sums[:, images].rearrange("p v t -> p (v t)"), ACT.Ln, bias=SHIFT**3 if lo == first_plain else 0.0)
+            nc.scalar.activation(plain_logs[:, images.start * PACK : images.stop * PACK], sums[:, images].rearrange("p v t -> p (v t)"), ACT.Ln, bias=SHIFT**3 if lo < V - BJ // D else 0.0)
 
         plain_ranges = [(320, 384), (384, 448), (448, 480), (480, 512)]
-        pool_pairs(0, 2, 0)
+        pool_pairs(0, 4, 0)
         floor_odd(5)
+        add_plain(*plain_ranges[0])
+        pool_pairs(4, 8, 1)
         floor_odd(6)
         floor_odd(7)
-        for images in plain_ranges:
+        for images in plain_ranges[1:]:
             add_plain(*images)
-        pool_pairs(2, 6, 1)
-        pool_pairs(6, 8, 2)
         plain_log(*plain_ranges[0])
-        pool_pairs(8, 10, 0)
+        pool_pairs(8, 10, 2)
         for images in plain_ranges[1:]:
             plain_log(*images)
         first_logs = bank(7, "first_logs")[:, 0, :]

@@ -1,5 +1,7 @@
 from contextlib import ExitStack
 
+import math
+
 import concourse.mybir as mybir
 from concourse.masks import make_identity
 
@@ -21,16 +23,17 @@ P = 128
 PACK = 4
 SHIFT = 0.05
 F32_MAX = 3.4028234663852886e38
-CHUNKS = 4
-CV = V // CHUNKS
-CJ = CV * D
 BJ = 128
-WARM_UP_COLUMNS = (512, 64)
-LINE = 4
-TURNED = 10
 BANKS = S // BJ
 TURN = P // PACK
-SPANS = V // P
+SPAN = 128
+SPANS = V // SPAN
+TURNED = 10
+WARM_UP_COLUMNS = (512, 64)
+LINE = 4
+MANTISSA = 0x007FFFFF
+ONE = 0x3F800000
+SIGN = -0x80000000
 
 
 def tile_picked_ygem_none_po_kernel(tc, x_words, x_scales, w1, w2, gain, offs, out_0, out_1, out_2):
@@ -38,9 +41,6 @@ def tile_picked_ygem_none_po_kernel(tc, x_words, x_scales, w1, w2, gain, offs, o
     with ExitStack() as ctx:
         keep = ctx.enter_context(tc.tile_pool(name="keep", bufs=1))
         psum = ctx.enter_context(tc.psum_pool(name="psum", bufs=1))
-
-        def bank(n, name):
-            return psum.tile([P, PACK, P], F32, name=name, tag=f"bank{n}")
 
         scale_table = keep.tile([P, T], U8, name="scale_table", align_bytes=64)
         nc.vector.memset(scale_table[:].bitcast(I32), 0)
@@ -50,6 +50,8 @@ def tile_picked_ygem_none_po_kernel(tc, x_words, x_scales, w1, w2, gain, offs, o
             nc.sync.dma_start(raw[:], w.rearrange("(p j) c -> p j c", j=PACK)[:, :, 256 * h : 256 * (h + 1)])
             return raw
 
+        gains = keep.tile([P, PACK], F32, name="gains")
+        nc.sync.dma_start(gains[:], gain.rearrange("(p t) o -> p (t o)", t=PACK))
         w1_raw = [load_half(w1, "w1", 0)]
         offsets = keep.tile([P, S // 16], U16, name="offsets")
         nc.sync.dma_start(offsets[:], offs)
@@ -60,13 +62,53 @@ def tile_picked_ygem_none_po_kernel(tc, x_words, x_scales, w1, w2, gain, offs, o
         nc.sync.dma_start(word_table[:].bitcast(I32), x_words[0].rearrange("p n r -> p (n r)").bitcast(I32))
         w2_raw = keep.tile([P, PACK, N], F32, name="w2_raw")
         nc.sync.dma_start(w2_raw[:], w2.rearrange("(p j) c -> p j c", j=PACK))
-        gains = keep.tile([P, PACK], F32, name="gains")
-        nc.sync.dma_start(gains[:], gain.rearrange("(p t) o -> p (t o)", t=PACK))
 
         ones = keep.tile([P, 1], F32, name="ones")
         nc.vector.memset(ones[:], 1.0)
         mean_bias = keep.tile([P, 1], F32, name="mean_bias")
         nc.scalar.activation(mean_bias[:], ones[:], ACT.Ln, scale=float(D) ** (-1.0 / 3.0))
+
+        identity = keep.tile([P, P], F32, name="identity")
+        make_identity(nc, identity[:])
+
+        bits = gains[:].bitcast(I32)
+        mantissas = keep.tile([P, PACK], I32, name="mantissas")
+        exponents = keep.tile([P, PACK], I32, name="exponents")
+        signs = keep.tile([P, PACK], I32, name="signs")
+        nc.vector.tensor_scalar(mantissas[:], bits, MANTISSA, ONE, ALU.bitwise_and, ALU.bitwise_or)
+        nc.vector.tensor_scalar(exponents[:], bits, 23, 0xFF, ALU.logical_shift_right, ALU.bitwise_and)
+        nc.vector.tensor_scalar(signs[:], bits, SIGN, ONE, ALU.bitwise_and, ALU.bitwise_or)
+        sizes = keep.tile([P, PACK], F32, name="sizes")
+        nc.vector.tensor_tensor(sizes[:], gains[:], signs[:].bitcast(F32), ALU.mult)
+        log_mantissas = keep.tile([P, PACK], F32, name="log_mantissas")
+        nc.scalar.activation(log_mantissas[:], mantissas[:].bitcast(F32), ACT.Ln)
+        log_powers = keep.tile([P, PACK], F32, name="log_powers")
+        nc.vector.tensor_scalar(log_powers[:], exponents[:], -127.0, 3.0 * math.log(2.0), ALU.add, ALU.mult)
+        log_gains = keep.tile([P, TURN, PACK], F32, name="log_gains")
+        nc.vector.scalar_tensor_tensor(
+            log_gains[:],
+            log_mantissas[:].unsqueeze(1).to_broadcast([P, TURN, PACK]),
+            3.0,
+            log_powers[:].unsqueeze(1).to_broadcast([P, TURN, PACK]),
+            ALU.mult,
+            ALU.add,
+        )
+        def bank(n, name):
+            return psum.tile([P, PACK, P], F32, name=name, tag=f"bank{n}")
+
+        turning = bank(7, "turning")
+        nc.tensor.transpose(turning[:, 0, :], log_gains[:].rearrange("p v t -> p (v t)"), identity[:])
+        turned_gains = keep.tile([P, P], F32, name="turned_gains")
+        nc.scalar.copy(turned_gains[:], turning[:, 0, :])
+        logs = []
+
+        def lay_gains(g):
+            logs.append(bank(g, f"logs{g}"))
+            for a in range(min(PACK, TURNED - g * PACK)):
+                nc.tensor.matmul(logs[g][:, a, :], turned_gains[:], identity[:], start=a == 0, stop=False, is_transpose=True)
+
+        lay_gains(0)
+        lay_gains(1)
 
         def deal(copy, grouped, raw, h, a, b):
             dst = grouped[:].rearrange("p (t m j) -> p m j t", t=PACK, j=PACK)[:, 64 * h + a : 64 * h + b]
@@ -88,8 +130,6 @@ def tile_picked_ygem_none_po_kernel(tc, x_words, x_scales, w1, w2, gain, offs, o
             nc.vector.tensor_copy(xc[:], word_table[:].indirect(offsets[:, lo // 16 : hi // 16]))
             x_code_tiles.extend(xc[:, at : at + BJ] for at in range(0, hi - lo, BJ))
 
-        identity = keep.tile([P, P], F32, name="identity")
-        make_identity(nc, identity[:])
         pieces = [(0, 1), (1, 3), (3, 4), (4, 5), (5, 6), (6, 7), (7, 8)]
         cube_tiles = {lo: keep.tile([P, (hi - lo) * BJ, PACK], F32, name=f"cubes{lo}", tag=f"cubes{lo}", align_bytes=64) for lo, hi in pieces}
         cubes = [cube_tiles[lo][:, (b - lo) * BJ : (b - lo + 1) * BJ] for lo, hi in pieces for b in range(lo, hi)]
@@ -97,7 +137,7 @@ def tile_picked_ygem_none_po_kernel(tc, x_words, x_scales, w1, w2, gain, offs, o
         turned_logs = keep.tile([P, TURNED * P], F32, name="turned_logs")
 
         def cube(b):
-            acc = bank(b, f"acc{b}")
+            acc = bank((2, 3, 4, 5, 6, 7, 3, 4)[b], f"acc{b}")
             for t in range(PACK):
                 nc.tensor.matmul_mx(
                     out=acc[:, t, :],
@@ -130,19 +170,18 @@ def tile_picked_ygem_none_po_kernel(tc, x_words, x_scales, w1, w2, gain, offs, o
                     nc.tensor.matmul(sums[:, a - lo, :], group, identity[:], start=e == 0, stop=e == D - 1, is_transpose=True)
             nc.scalar.activation(turned_logs[:, lo * P : hi * P], sums[:, : hi - lo, :].rearrange("p a c -> p (a c)"), ACT.Ln, bias=bias)
 
-        logs = []
-
         def turn_back(g):
-            logs.append(bank(3 + g, f"logs{g}"))
-            for a in range(min(PACK, TURNED - g * PACK)):
+            count = min(PACK, TURNED - g * PACK)
+            for a in range(count):
                 at = (g * PACK + a) * P
-                nc.tensor.transpose(logs[g][:, a, :] if at else first_logs, turned_logs[:, at : at + P], identity[:])
+                nc.tensor.matmul(logs[g][:, a, :], turned_logs[:, at : at + P], identity[:], start=False, stop=a == count - 1, is_transpose=True)
 
         for b in range(BANKS):
             cube(b)
             if b in (0, 2, 3, 4):
                 lo, hi = 2 if b == 2 else 2 * b, 2 * b + 2
                 floor(lo, hi, floored_tile(lo, hi, f"floored{b}"))
+        lay_gains(2)
         first_plain = TURNED * TURN
         scalar_odds = keep.tile([P, 2, BJ // D, PACK], F32, name="scalar_odds")
         late = keep.tile([P, 4, BJ // D, PACK], F32, name="late", tag="pooled", align_bytes=64)
@@ -168,40 +207,48 @@ def tile_picked_ygem_none_po_kernel(tc, x_words, x_scales, w1, w2, gain, offs, o
             nc.scalar.activation(plain_logs[:, images.start * PACK : images.stop * PACK], sums[:, images].rearrange("p v t -> p (v t)"), ACT.Ln, bias=SHIFT**3 if lo < V - BJ // D else 0.0)
 
         plain_ranges = [(320, 384), (384, 448), (448, 480), (480, 512)]
-        pool_pairs(0, 4, 0)
+        pool_pairs(0, 4, 5)
         floor_odd(5)
         add_plain(*plain_ranges[0])
-        pool_pairs(4, 8, 1)
+        pool_pairs(4, 8, 6)
         floor_odd(6)
         floor_odd(7)
         for images in plain_ranges[1:]:
             add_plain(*images)
         plain_log(*plain_ranges[0])
-        pool_pairs(8, 10, 2)
+        pool_pairs(8, 10, 7)
         for images in plain_ranges[1:]:
             plain_log(*images)
-        first_logs = bank(7, "first_logs")[:, 0, :]
         for g in range(3):
             turn_back(g)
 
-        w2_bf = keep.tile([P, PACK * N], BF16, name="w2_bf", tag="cubes7", align_bytes=64)
+        w2_bf = keep.tile([P, PACK * N], BF16, name="w2_bf", tag="cubes6", align_bytes=64)
         w2_codes = keep.tile([P, N], U32, name="w2_codes", align_bytes=64)
         w2_scales = keep.tile([P, N], U8, name="w2_scales", align_bytes=64)
         w2_dst = w2_bf[:].rearrange("p (t m j) -> p m j t", t=PACK, j=PACK)
         w2_src = w2_raw[:].rearrange("p j (m t) -> p m j t", t=PACK)
+        row_signs = signs[:].bitcast(F32).unsqueeze(1).unsqueeze(3)
+
+        def round_w2(lo, hi, first):
+            nc.vector.tensor_tensor(
+                w2_dst[:, lo:hi, :, first : first + 2],
+                w2_src[:, lo:hi, :, first : first + 2],
+                row_signs.to_broadcast([P, hi - lo, PACK, 2]),
+                ALU.mult,
+            )
 
         def quantise_w2(lo, hi):
             nc.vector.quantize_mx(out=w2_codes[:, lo:hi].bitcast(FP8X4), scales=w2_scales[:, lo:hi], in_=w2_bf[:, lo * PACK : hi * PACK])
 
-        nc.vector.tensor_copy(w2_dst[:, :, :, 0:2], w2_src[:, :, :, 0:2])
-        nc.vector.tensor_copy(w2_dst[:, :64, :, 2:4], w2_src[:, :64, :, 2:4])
+        round_w2(0, P, 0)
+        round_w2(0, 64, 2)
         quantise_w2(0, 2 * P)
-        nc.vector.tensor_copy(w2_dst[:, 64:, :, 2:4], w2_src[:, 64:, :, 2:4])
+        round_w2(64, P, 2)
         for half in range(2):
             for t in (2, 3):
                 quantise_w2(t * P + 64 * half, t * P + 64 * (half + 1))
 
-        idle = bank(7, "idle")[:].rearrange("p a c -> p (a c)")
+        idle = bank(3, "idle")[:].rearrange("p a c -> p (a c)")
         for width in WARM_UP_COLUMNS:
             nc.tensor.matmul_mx(
                 out=idle[:, :width],
@@ -213,99 +260,98 @@ def tile_picked_ygem_none_po_kernel(tc, x_words, x_scales, w1, w2, gain, offs, o
                 stop=True,
             )
 
-        roots = keep.tile([P, V * PACK], F32, name="roots", tag="pooled", align_bytes=64)
+        roots = keep.tile([P, (V - first_plain) * PACK], F32, name="roots", tag="cubes7", align_bytes=64)
         out_scales = keep.tile([P, V], U8, name="out_scales", align_bytes=64)
         out_rows = out_0.rearrange("(p t) v -> p t v", t=PACK)
         out_words = out_1[0].rearrange("p c r -> p (c r)")
-        edges = [0, 128, 256, 384, 448, 512]
-        spans = list(zip(edges[:-1], edges[1:]))
-        z_all = keep.tile([P, V * PACK], BF16, name="z_all", align_bytes=64)
-        tail_lo = spans[3][0]
-        res_tail = keep.tile([P, PACK, V - tail_lo], F32, name="res_tail")
-        res = [keep.tile([P, PACK, hi - lo], F32, name=f"res{lo}")[:] for lo, hi in spans[:3]]
-        res.extend(res_tail[:, :, lo - tail_lo : hi - tail_lo] for lo, hi in spans[3:])
+        z_all = keep.tile([P, V * PACK], BF16, name="z_all", tag="pooled", align_bytes=64)
+        res = [keep.tile([P, PACK, SPAN], F32, name=f"res{g}") for g in range(SPANS)]
         res_bf = keep.tile([P, V * PACK], BF16, name="res_bf", align_bytes=64)
-
-        last = len(spans) - 1
+        codes = [keep.tile([P, V // 2], U32, name=f"out_codes{half}", align_bytes=64) for half in range(2)]
 
         def root(lo, hi):
-            cols = slice(lo * PACK, hi * PACK)
-            if lo == 0:
-                source = first_logs
-            elif lo < first_plain:
+            if lo < first_plain:
                 source = logs[lo // P][:].rearrange("p g c -> p (g c)")[:, lo % P * PACK : (lo % P + hi - lo) * PACK]
+                target = z_all[:, lo * PACK : hi * PACK]
             else:
-                source = plain_logs[:, (lo - first_plain) * PACK : (hi - first_plain) * PACK]
-            nc.scalar.activation(roots[:, cols], source, ACT.Exp, bias=mean_bias[:], scale=1.0 / 3.0)
+                cols = slice((lo - first_plain) * PACK, (hi - first_plain) * PACK)
+                source, target = plain_logs[:, cols], roots[:, cols]
+            nc.scalar.activation(target, source, ACT.Exp, bias=mean_bias[:], scale=1.0 / 3.0)
 
         def apply_gain(lo, hi):
-            cols = slice(lo * PACK, hi * PACK)
             nc.vector.tensor_tensor(
-                z_all[:, cols].rearrange("p (v t) -> p v t", t=PACK),
-                roots[:, cols].rearrange("p (v t) -> p v t", t=PACK),
-                gains[:].unsqueeze(1).to_broadcast([P, hi - lo, PACK]),
+                z_all[:, lo * PACK : hi * PACK].rearrange("p (v t) -> p v t", t=PACK),
+                roots[:, (lo - first_plain) * PACK : (hi - first_plain) * PACK].rearrange("p (v t) -> p v t", t=PACK),
+                sizes[:].unsqueeze(1).to_broadcast([P, hi - lo, PACK]),
                 ALU.mult,
             )
 
-        def whiten(lo, hi):
-            zc = keep.tile([P, hi - lo], U32, name=f"zc{lo}", align_bytes=64)
-            zs = keep.tile([P, hi - lo], U8, name=f"zs{lo}", align_bytes=64)
+        def whiten(g, banks):
+            lo, hi = g * SPAN, (g + 1) * SPAN
+            zc = keep.tile([P, SPAN], U32, name=f"zc{g}", align_bytes=64)
+            zs = keep.tile([P, SPAN], U8, name=f"zs{g}", align_bytes=64)
             nc.vector.quantize_mx(out=zc[:].bitcast(FP8X4), scales=zs[:], in_=z_all[:, lo * PACK : hi * PACK])
-            per_bank = 2 if lo == 0 else PACK
-            for first in range(0, PACK, per_bank):
-                acc = bank((0, 1, 2, 6, 7)[lo // P + (lo + first > 0)], f"product{lo}")[:, :per_bank, :]
-                for t in range(first, first + per_bank):
-                    nc.tensor.matmul_mx(
-                        out=acc[:, t - first, :],
-                        lhsT=w2_codes[:, t * P : (t + 1) * P].bitcast(FP8X4),
-                        lhsT_scale=w2_scales[:, t * P : (t + 1) * P],
-                        rhs=zc[:].bitcast(FP8X4),
-                        rhs_scale=zs[:],
-                        start=True,
-                        stop=True,
-                    )
-                if hi < V:
-                    nc.scalar.copy(res[lo // P][:, first : first + per_bank], acc)
-            if hi < V:
-                nc.sync.dma_start(out_rows[:, :, lo:hi], res[lo // P])
-            else:
-                for c in (last - 1, last):
-                    nc.scalar.copy(res[c], acc[:, :, spans[c][0] - lo : spans[c][1] - lo])
-                nc.sync.dma_start(out_rows[:, :, tail_lo:V], res_tail[:])
-                weave(nc.scalar.copy, last, acc[:, :, spans[last][0] - lo :])
+            per_bank = PACK // len(banks)
+            accs = [bank(n, f"product{g}")[:, :per_bank, :] for n in banks]
+            for t in range(PACK):
+                nc.tensor.matmul_mx(
+                    out=accs[t // per_bank][:, t % per_bank, :],
+                    lhsT=w2_codes[:, t * P : (t + 1) * P].bitcast(FP8X4),
+                    lhsT_scale=w2_scales[:, t * P : (t + 1) * P],
+                    rhs=zc[:].bitcast(FP8X4),
+                    rhs_scale=zs[:],
+                    start=True,
+                    stop=True,
+                )
+            return accs
 
-        def weave(copy, c, source):
-            lo, hi = spans[c]
+        def store(g):
+            nc.sync.dma_start(out_rows[:, :, g * SPAN : (g + 1) * SPAN], res[g][:])
+
+        def weave(copy, lo, hi, source):
             target = res_bf[:, lo * PACK : hi * PACK].rearrange("p (c i t) -> p c t i", t=PACK, i=LINE)
             copy(target, source.rearrange("p t (c i) -> p c t i", i=LINE))
 
-        split = spans[3][0]
-        early_codes = keep.tile([P, split], U32, name="early_codes", align_bytes=64)
-        late_codes = keep.tile([P, V - split], U32, name="late_codes", align_bytes=64)
-
-        def hand_on(c):
-            lo, hi = spans[c]
-            codes, first = (early_codes, 0) if hi <= split else (late_codes, split)
+        def hand_on(lo, hi):
+            half, at = divmod(lo, V // 2)
             nc.vector.quantize_mx(
-                out=codes[:, lo - first : hi - first].bitcast(FP8X4), scales=out_scales[:, lo:hi], in_=res_bf[:, lo * PACK : hi * PACK]
+                out=codes[half][:, at : at + hi - lo].bitcast(FP8X4), scales=out_scales[:, lo:hi], in_=res_bf[:, lo * PACK : hi * PACK]
             )
-            if c in (2, 3):
-                nc.sync.dma_start(out_words[:, first * PACK : (first + codes.shape[1]) * PACK].bitcast(I32), codes[:].bitcast(I32))
 
-        pieces_of_roots = [(0, 32), (32, 64)] + [(lo, lo + 64) for lo in range(64, V, 64)]
-        for lo, hi in pieces_of_roots:
+        def store_codes(half):
+            nc.sync.dma_start(out_words[:, half * V * 2 : (half + 1) * V * 2].bitcast(I32), codes[half][:].bitcast(I32))
+
+        plain_pieces = [(lo, lo + 64) for lo in range(first_plain, V, 64)]
+        for lo, hi in [(0, P)] + plain_pieces + [(2 * P, first_plain), (P, 2 * P)]:
             root(lo, hi)
-        for lo, hi in pieces_of_roots:
-            apply_gain(lo, hi)
-            if lo > 0 and lo % P == 0:
-                whiten(lo - P, lo)
-        whiten(V - P, V)
-        for c in range(last):
-            weave(nc.vector.tensor_copy, c, res[c])
-            if c > 0:
-                hand_on(c - 1)
-        hand_on(last)
-        hand_on(last - 1)
+        first = whiten(0, (4, 5))
+        for piece in plain_pieces:
+            apply_gain(*piece)
+        third = whiten(2, (6,))
+        fourth = whiten(3, (7,))
+        nc.vector.tensor_copy(res[0][:, :2], first[0])
+        second = whiten(1, (3,))
+        nc.vector.tensor_copy(res[0][:, 2:], first[1])
+        store(0)
+        nc.scalar.copy(res[2][:], third[0])
+        store(2)
+        nc.scalar.copy(res[3][:], fourth[0])
+        store(3)
+        middle = SPAN + SPAN // 2
+        nc.scalar.copy(res[1][:, :, : SPAN // 2], second[0][:, :, : SPAN // 2])
+        nc.scalar.copy(res[1][:, :, SPAN // 2 :], second[0][:, :, SPAN // 2 :])
+        store(1)
+        weave(nc.scalar.copy, middle, 2 * SPAN, second[0][:, :, SPAN // 2 :])
+        weave(nc.vector.tensor_copy, 0, SPAN, res[0][:])
+        weave(nc.vector.tensor_copy, 2 * SPAN, 3 * SPAN, res[2][:])
+        hand_on(0, SPAN)
+        weave(nc.vector.tensor_copy, 3 * SPAN, V, res[3][:])
+        hand_on(2 * SPAN, 3 * SPAN)
+        weave(nc.vector.tensor_copy, SPAN, middle, res[1][:, :, : SPAN // 2])
+        hand_on(3 * SPAN, V)
+        store_codes(1)
+        hand_on(SPAN, 2 * SPAN)
+        store_codes(0)
 
         for q in range(4):
             queue = nc.scalar if q % 2 else nc.sync

from contextlib import ExitStack

import math

import concourse.mybir as mybir
from concourse.masks import make_identity

K, T, S, H, N, D = 512, 2048, 1024, 512, 512, 2
V = S // D
FLOPS = 2 * K * H * S + 2 * H * N * V

F32 = mybir.dt.float32
BF16 = mybir.dt.bfloat16
I32 = mybir.dt.int32
U32 = mybir.dt.uint32
U16 = mybir.dt.uint16
U8 = mybir.dt.uint8
FP8X4 = mybir.dt.float8_e4m3fn_x4
ACT = mybir.ActivationFunctionType
ALU = mybir.AluOpType

P = 128
PACK = 4
SHIFT = 0.05
F32_MAX = 3.4028234663852886e38
BJ = 128
BANKS = S // BJ
TURN = P // PACK
SPAN = 128
SPANS = V // SPAN
TURNED = 10
WARM_UP_COLUMNS = (512, 64)
LINE = 4
MANTISSA = 0x007FFFFF
ONE = 0x3F800000
SIGN = -0x80000000


def tile_picked_ygem_none_po_kernel(tc, x_words, x_scales, w1, w2, gain, offs, out_0, out_1, out_2):
    nc = tc.nc
    with ExitStack() as ctx:
        keep = ctx.enter_context(tc.tile_pool(name="keep", bufs=1))
        psum = ctx.enter_context(tc.psum_pool(name="psum", bufs=1))

        scale_table = keep.tile([P, T], U8, name="scale_table", align_bytes=64)
        nc.vector.memset(scale_table[:].bitcast(I32), 0)

        def load_half(w, name, h):
            raw = keep.tile([P, PACK, 256], F32, name=f"{name}_raw{h}")
            nc.sync.dma_start(raw[:], w.rearrange("(p j) c -> p j c", j=PACK)[:, :, 256 * h : 256 * (h + 1)])
            return raw

        gains = keep.tile([P, PACK], F32, name="gains")
        nc.sync.dma_start(gains[:], gain.rearrange("(p t) o -> p (t o)", t=PACK))
        w1_raw = [load_half(w1, "w1", 0)]
        offsets = keep.tile([P, S // 16], U16, name="offsets")
        nc.sync.dma_start(offsets[:], offs)
        for q in range(4):
            nc.sync.dma_start(scale_table[32 * q : 32 * q + 4, :].bitcast(I32), x_scales[0, 4 * q : 4 * q + 4, :].bitcast(I32))
        w1_raw.append(load_half(w1, "w1", 1))
        word_table = keep.tile([P, T], U32, name="word_table", align_bytes=64)
        nc.sync.dma_start(word_table[:].bitcast(I32), x_words[0].rearrange("p n r -> p (n r)").bitcast(I32))
        w2_raw = keep.tile([P, PACK, N], F32, name="w2_raw")
        nc.sync.dma_start(w2_raw[:], w2.rearrange("(p j) c -> p j c", j=PACK))

        ones = keep.tile([P, 1], F32, name="ones")
        nc.vector.memset(ones[:], 1.0)
        mean_bias = keep.tile([P, 1], F32, name="mean_bias")
        nc.scalar.activation(mean_bias[:], ones[:], ACT.Ln, scale=float(D) ** (-1.0 / 3.0))

        identity = keep.tile([P, P], F32, name="identity")
        make_identity(nc, identity[:])

        bits = gains[:].bitcast(I32)
        mantissas = keep.tile([P, PACK], I32, name="mantissas")
        exponents = keep.tile([P, PACK], I32, name="exponents")
        signs = keep.tile([P, PACK], I32, name="signs")
        nc.vector.tensor_scalar(mantissas[:], bits, MANTISSA, ONE, ALU.bitwise_and, ALU.bitwise_or)
        nc.vector.tensor_scalar(exponents[:], bits, 23, 0xFF, ALU.logical_shift_right, ALU.bitwise_and)
        nc.vector.tensor_scalar(signs[:], bits, SIGN, ONE, ALU.bitwise_and, ALU.bitwise_or)
        sizes = keep.tile([P, PACK], F32, name="sizes")
        nc.vector.tensor_tensor(sizes[:], gains[:], signs[:].bitcast(F32), ALU.mult)
        log_mantissas = keep.tile([P, PACK], F32, name="log_mantissas")
        nc.scalar.activation(log_mantissas[:], mantissas[:].bitcast(F32), ACT.Ln)
        log_powers = keep.tile([P, PACK], F32, name="log_powers")
        nc.vector.tensor_scalar(log_powers[:], exponents[:], -127.0, 3.0 * math.log(2.0), ALU.add, ALU.mult)
        log_gains = keep.tile([P, TURN, PACK], F32, name="log_gains")
        nc.vector.scalar_tensor_tensor(
            log_gains[:],
            log_mantissas[:].unsqueeze(1).to_broadcast([P, TURN, PACK]),
            3.0,
            log_powers[:].unsqueeze(1).to_broadcast([P, TURN, PACK]),
            ALU.mult,
            ALU.add,
        )
        def bank(n, name):
            return psum.tile([P, PACK, P], F32, name=name, tag=f"bank{n}")

        turning = bank(7, "turning")
        nc.tensor.transpose(turning[:, 0, :], log_gains[:].rearrange("p v t -> p (v t)"), identity[:])
        turned_gains = keep.tile([P, P], F32, name="turned_gains")
        nc.scalar.copy(turned_gains[:], turning[:, 0, :])
        logs = []

        def lay_gains(g):
            logs.append(bank(g, f"logs{g}"))
            for a in range(min(PACK, TURNED - g * PACK)):
                nc.tensor.matmul(logs[g][:, a, :], turned_gains[:], identity[:], start=a == 0, stop=False, is_transpose=True)

        lay_gains(0)
        lay_gains(1)

        def deal(copy, grouped, raw, h, a, b):
            dst = grouped[:].rearrange("p (t m j) -> p m j t", t=PACK, j=PACK)[:, 64 * h + a : 64 * h + b]
            src = raw[:].rearrange("p j (m t) -> p m j t", t=PACK)[:, a:b]
            copy(dst, src)

        picked_scales = keep.tile([P, S], U8, name="picked_scales", align_bytes=64)
        nc.vector.tensor_copy(picked_scales[:], scale_table[:].indirect(offsets[:]))
        w1_bf = keep.tile([P, PACK * H], BF16, name="w1_bf", align_bytes=64)
        deal(nc.scalar.copy, w1_bf, w1_raw[0], 0, 0, 64)
        deal(nc.scalar.copy, w1_bf, w1_raw[1], 1, 0, 64)
        w1_codes = keep.tile([P, H], U32, name="w1_codes", align_bytes=64)
        w1_scales = keep.tile([P, H], U8, name="w1_scales", align_bytes=64)
        nc.vector.quantize_mx(out=w1_codes[:].bitcast(FP8X4), scales=w1_scales[:], in_=w1_bf[:])

        x_code_tiles = []
        for lo, hi in [(0, 128), (128, 384), (384, 1024)]:
            xc = keep.tile([P, hi - lo], U32, name=f"xc{lo}", align_bytes=64)
            nc.vector.tensor_copy(xc[:], word_table[:].indirect(offsets[:, lo // 16 : hi // 16]))
            x_code_tiles.extend(xc[:, at : at + BJ] for at in range(0, hi - lo, BJ))

        pieces = [(0, 1), (1, 3), (3, 4), (4, 5), (5, 6), (6, 7), (7, 8)]
        cube_tiles = {lo: keep.tile([P, (hi - lo) * BJ, PACK], F32, name=f"cubes{lo}", tag=f"cubes{lo}", align_bytes=64) for lo, hi in pieces}
        cubes = [cube_tiles[lo][:, (b - lo) * BJ : (b - lo + 1) * BJ] for lo, hi in pieces for b in range(lo, hi)]
        floored = {}
        turned_logs = keep.tile([P, TURNED * P], F32, name="turned_logs")

        def cube(b):
            acc = bank((2, 3, 4, 5, 6, 7, 3, 4)[b], f"acc{b}")
            for t in range(PACK):
                nc.tensor.matmul_mx(
                    out=acc[:, t, :],
                    lhsT=w1_codes[:, t * P : (t + 1) * P].bitcast(FP8X4),
                    lhsT_scale=w1_scales[:, t * P : (t + 1) * P],
                    rhs=x_code_tiles[b].bitcast(FP8X4),
                    rhs_scale=picked_scales[:, b * BJ : (b + 1) * BJ],
                    start=True,
                    stop=True,
                )
            woven = acc[:].rearrange("p t j -> p j t")
            sq = keep.tile([P, BJ, PACK], F32, name=f"sq{b}", tag=f"sq{b}" if b < BANKS - 1 else "pooled", align_bytes=64)
            nc.scalar.activation(sq[:], woven, ACT.Square, bias=SHIFT)
            nc.vector.scalar_tensor_tensor(cubes[b], woven, SHIFT, sq[:], ALU.add, ALU.mult)

        def floor(lo, hi, tile):
            pairs = cube_tiles[lo // 2][:].rearrange("p (v e) t -> p e v t", e=D)
            for a in range(lo, hi):
                floored[a] = tile[:, :, (a - lo) * TURN : (a - lo + 1) * TURN]
            nc.gpsimd.tensor_scalar(tile, pairs, F32_MAX, SHIFT**3, ALU.min, ALU.max)

        def floored_tile(lo, hi, tag):
            return keep.tile([P, D, (hi - lo) * TURN, PACK], F32, name=f"floored{lo}", tag=tag, align_bytes=64)[:]

        def pool_pairs(lo, hi, n, bias=0.0):
            sums = bank(n, f"sums{lo}")
            for a in range(lo, hi):
                for e in range(D):
                    group = floored[a][:, e].rearrange("p v t -> p (v t)")
                    nc.tensor.matmul(sums[:, a - lo, :], group, identity[:], start=e == 0, stop=e == D - 1, is_transpose=True)
            nc.scalar.activation(turned_logs[:, lo * P : hi * P], sums[:, : hi - lo, :].rearrange("p a c -> p (a c)"), ACT.Ln, bias=bias)

        def turn_back(g):
            count = min(PACK, TURNED - g * PACK)
            for a in range(count):
                at = (g * PACK + a) * P
                nc.tensor.matmul(logs[g][:, a, :], turned_logs[:, at : at + P], identity[:], start=False, stop=a == count - 1, is_transpose=True)

        for b in range(BANKS):
            cube(b)
            if b in (0, 2, 3, 4):
                lo, hi = 2 if b == 2 else 2 * b, 2 * b + 2
                floor(lo, hi, floored_tile(lo, hi, f"floored{b}"))
        lay_gains(2)
        first_plain = TURNED * TURN
        scalar_odds = keep.tile([P, 2, BJ // D, PACK], F32, name="scalar_odds")
        late = keep.tile([P, 4, BJ // D, PACK], F32, name="late", tag="pooled", align_bytes=64)
        odds = {5: scalar_odds[:, 0], 6: scalar_odds[:, 1], 7: late[:, 0]}
        sums = late[:, 1:].rearrange("p b v t -> p (b v) t")
        plain_logs = keep.tile([P, (V - first_plain) * PACK], F32, name="plain_logs")

        def floor_odd(b):
            pairs = cubes[b].rearrange("p (v e) t -> p v e t", e=D)
            if b < BANKS - 1:
                nc.scalar.activation(odds[b], pairs[:, :, 1, :], ACT.Relu, bias=-(SHIFT**3))
            else:
                nc.vector.tensor_scalar(odds[b], pairs[:, :, 1, :], SHIFT**3, None, ALU.max)

        def add_plain(lo, hi):
            b, at = divmod(lo, BJ // D)
            pairs = cubes[b].rearrange("p (v e) t -> p v e t", e=D)[:, at : at + hi - lo]
            images = slice(lo - first_plain, hi - first_plain)
            nc.vector.scalar_tensor_tensor(sums[:, images], pairs[:, :, 0, :], SHIFT**3, odds[b][:, at : at + hi - lo], ALU.max, ALU.add)

        def plain_log(lo, hi):
            images = slice(lo - first_plain, hi - first_plain)
            nc.scalar.activation(plain_logs[:, images.start * PACK : images.stop * PACK], sums[:, images].rearrange("p v t -> p (v t)"), ACT.Ln, bias=SHIFT**3 if lo < V - BJ // D else 0.0)

        plain_ranges = [(320, 384), (384, 448), (448, 480), (480, 512)]
        pool_pairs(0, 4, 5)
        floor_odd(5)
        add_plain(*plain_ranges[0])
        pool_pairs(4, 8, 6)
        floor_odd(6)
        floor_odd(7)
        for images in plain_ranges[1:]:
            add_plain(*images)
        plain_log(*plain_ranges[0])
        pool_pairs(8, 10, 7)
        for images in plain_ranges[1:]:
            plain_log(*images)
        for g in range(3):
            turn_back(g)

        w2_bf = keep.tile([P, PACK * N], BF16, name="w2_bf", tag="cubes6", align_bytes=64)
        w2_codes = keep.tile([P, N], U32, name="w2_codes", align_bytes=64)
        w2_scales = keep.tile([P, N], U8, name="w2_scales", align_bytes=64)
        w2_dst = w2_bf[:].rearrange("p (t m j) -> p m j t", t=PACK, j=PACK)
        w2_src = w2_raw[:].rearrange("p j (m t) -> p m j t", t=PACK)
        row_signs = signs[:].bitcast(F32).unsqueeze(1).unsqueeze(3)

        def round_w2(lo, hi, first):
            nc.vector.tensor_tensor(
                w2_dst[:, lo:hi, :, first : first + 2],
                w2_src[:, lo:hi, :, first : first + 2],
                row_signs.to_broadcast([P, hi - lo, PACK, 2]),
                ALU.mult,
            )

        def quantise_w2(lo, hi):
            nc.vector.quantize_mx(out=w2_codes[:, lo:hi].bitcast(FP8X4), scales=w2_scales[:, lo:hi], in_=w2_bf[:, lo * PACK : hi * PACK])

        round_w2(0, P, 0)
        round_w2(0, 64, 2)
        quantise_w2(0, 2 * P)
        round_w2(64, P, 2)
        for half in range(2):
            for t in (2, 3):
                quantise_w2(t * P + 64 * half, t * P + 64 * (half + 1))

        idle = bank(3, "idle")[:].rearrange("p a c -> p (a c)")
        for width in WARM_UP_COLUMNS:
            nc.tensor.matmul_mx(
                out=idle[:, :width],
                lhsT=w2_codes[:, N - P :].bitcast(FP8X4),
                lhsT_scale=w2_scales[:, N - P :],
                rhs=w1_codes[:, :width].bitcast(FP8X4),
                rhs_scale=w1_scales[:, :width],
                start=True,
                stop=True,
            )

        roots = keep.tile([P, (V - first_plain) * PACK], F32, name="roots", tag="cubes7", align_bytes=64)
        out_scales = keep.tile([P, V], U8, name="out_scales", align_bytes=64)
        out_rows = out_0.rearrange("(p t) v -> p t v", t=PACK)
        out_words = out_1[0].rearrange("p c r -> p (c r)")
        z_all = keep.tile([P, V * PACK], BF16, name="z_all", tag="pooled", align_bytes=64)
        res = [keep.tile([P, PACK, SPAN], F32, name=f"res{g}") for g in range(SPANS)]
        res_bf = keep.tile([P, V * PACK], BF16, name="res_bf", align_bytes=64)
        codes = [keep.tile([P, V // 2], U32, name=f"out_codes{half}", align_bytes=64) for half in range(2)]

        def root(lo, hi):
            if lo < first_plain:
                source = logs[lo // P][:].rearrange("p g c -> p (g c)")[:, lo % P * PACK : (lo % P + hi - lo) * PACK]
                target = z_all[:, lo * PACK : hi * PACK]
            else:
                cols = slice((lo - first_plain) * PACK, (hi - first_plain) * PACK)
                source, target = plain_logs[:, cols], roots[:, cols]
            nc.scalar.activation(target, source, ACT.Exp, bias=mean_bias[:], scale=1.0 / 3.0)

        def apply_gain(lo, hi):
            nc.vector.tensor_tensor(
                z_all[:, lo * PACK : hi * PACK].rearrange("p (v t) -> p v t", t=PACK),
                roots[:, (lo - first_plain) * PACK : (hi - first_plain) * PACK].rearrange("p (v t) -> p v t", t=PACK),
                sizes[:].unsqueeze(1).to_broadcast([P, hi - lo, PACK]),
                ALU.mult,
            )

        def whiten(g, banks):
            lo, hi = g * SPAN, (g + 1) * SPAN
            zc = keep.tile([P, SPAN], U32, name=f"zc{g}", align_bytes=64)
            zs = keep.tile([P, SPAN], U8, name=f"zs{g}", align_bytes=64)
            nc.vector.quantize_mx(out=zc[:].bitcast(FP8X4), scales=zs[:], in_=z_all[:, lo * PACK : hi * PACK])
            per_bank = PACK // len(banks)
            accs = [bank(n, f"product{g}")[:, :per_bank, :] for n in banks]
            for t in range(PACK):
                nc.tensor.matmul_mx(
                    out=accs[t // per_bank][:, t % per_bank, :],
                    lhsT=w2_codes[:, t * P : (t + 1) * P].bitcast(FP8X4),
                    lhsT_scale=w2_scales[:, t * P : (t + 1) * P],
                    rhs=zc[:].bitcast(FP8X4),
                    rhs_scale=zs[:],
                    start=True,
                    stop=True,
                )
            return accs

        def store(g):
            nc.sync.dma_start(out_rows[:, :, g * SPAN : (g + 1) * SPAN], res[g][:])

        def weave(copy, lo, hi, source):
            target = res_bf[:, lo * PACK : hi * PACK].rearrange("p (c i t) -> p c t i", t=PACK, i=LINE)
            copy(target, source.rearrange("p t (c i) -> p c t i", i=LINE))

        def hand_on(lo, hi):
            half, at = divmod(lo, V // 2)
            nc.vector.quantize_mx(
                out=codes[half][:, at : at + hi - lo].bitcast(FP8X4), scales=out_scales[:, lo:hi], in_=res_bf[:, lo * PACK : hi * PACK]
            )

        def store_codes(half):
            nc.sync.dma_start(out_words[:, half * V * 2 : (half + 1) * V * 2].bitcast(I32), codes[half][:].bitcast(I32))

        plain_pieces = [(lo, lo + 64) for lo in range(first_plain, V, 64)]
        for lo, hi in [(0, P)] + plain_pieces + [(2 * P, first_plain), (P, 2 * P)]:
            root(lo, hi)
        first = whiten(0, (4, 5))
        for piece in plain_pieces:
            apply_gain(*piece)
        third = whiten(2, (6,))
        fourth = whiten(3, (7,))
        nc.vector.tensor_copy(res[0][:, :2], first[0])
        second = whiten(1, (3,))
        nc.vector.tensor_copy(res[0][:, 2:], first[1])
        store(0)
        nc.scalar.copy(res[2][:], third[0])
        store(2)
        nc.scalar.copy(res[3][:], fourth[0])
        store(3)
        middle = SPAN + SPAN // 2
        nc.scalar.copy(res[1][:, :, : SPAN // 2], second[0][:, :, : SPAN // 2])
        nc.scalar.copy(res[1][:, :, SPAN // 2 :], second[0][:, :, SPAN // 2 :])
        store(1)
        weave(nc.scalar.copy, middle, 2 * SPAN, second[0][:, :, SPAN // 2 :])
        weave(nc.vector.tensor_copy, 0, SPAN, res[0][:])
        weave(nc.vector.tensor_copy, 2 * SPAN, 3 * SPAN, res[2][:])
        hand_on(0, SPAN)
        weave(nc.vector.tensor_copy, 3 * SPAN, V, res[3][:])
        hand_on(2 * SPAN, 3 * SPAN)
        weave(nc.vector.tensor_copy, SPAN, middle, res[1][:, :, : SPAN // 2])
        hand_on(3 * SPAN, V)
        store_codes(1)
        hand_on(SPAN, 2 * SPAN)
        store_codes(0)

        for q in range(4):
            queue = nc.scalar if q % 2 else nc.sync
            queue.dma_start(out_2[0, 4 * q : 4 * q + 4, :].bitcast(I32), out_scales[32 * q : 32 * q + 4, :].bitcast(I32))
